import numpy as np, ml_dtypes
CORES = [1,5,17,21,33,37,49,53]
N = 8
BF = ml_dtypes.bfloat16
def f(rng, *shape):
    return (rng.standard_normal(shape, dtype=np.float32) * np.exp2(rng.integers(-2, 3, shape[:-1] + (1,)))).astype(BF)
def wide(rng, *shape):
    v = f(rng, *shape).astype(np.float32); k = shape[:-2] + (1, shape[-1])
    return (v * np.exp2(rng.integers(-6, 7, k)) * (rng.random(k) > 0.0625)).astype(BF)
def entries(a):
    return np.ascontiguousarray(a.T).reshape(-1)
def table(e):
    return np.ascontiguousarray(np.reshape(e, (-1, 16)).T).astype(np.int32)
K, V, A, R = 4096, 8192, 4096, 512
CAP, U, HS, AS = 96, 192, 3, 4
TM = 1048576
def fine(rng, v):
    return v.astype(np.float32) * (1 + rng.random(v.shape, dtype=np.float32))
def moments(rng, uneven, *shape):
    return np.floor(np.exp2(rng.random(shape) * 20)).astype(np.int64) - 1 if uneven else rng.integers(0, TM, shape)
def owners(rng, without=-1):
    return np.stack([rng.permutation(np.repeat(np.array([q for q in range(N) if q != without]), CAP))[:R] for r in range(N)])
def full(rng):
    o = []
    for r in range(N):
        a, b = (r + 1) % N, (r + 2) % N
        rest = rng.permutation(np.repeat(np.array([q for q in range(N) if q != a and q != b]), CAP))[:R - 2 * CAP]
        o.append(rng.permutation(np.concatenate([np.repeat(np.array([a, b]), CAP), rest])))
    return np.stack(o)
def make(rng, own, key, fall=True, share=False, edge=False, low=None, uneven=False):
    tt = moments(rng, uneven, N, 8, K, HS + AS)
    if fall: tt = -np.sort(-tt, axis=3)
    if low is not None: tt = tt // 2; tt[..., :HS] += TM // 2
    h = rng.integers(0, HS + 1, (N, 8, K))
    if edge: h = HS * rng.integers(0, 2, (N, 8, K)); h[:, :, :2] = HS
    ch = rng.integers(0, K, (N, 8, K)) if share else np.zeros((N, 8, K), np.int64) + np.arange(K)
    col, s = rng.integers(0, 8, (N, R)), rng.integers(0, HS + AS, (N, R)); tie = tt[own, col, ch[own, col, key], s]; u = rng.random((N, R))
    if edge: t = np.where(u < 0.2, 0, np.where(u < 0.4, TM - 1, np.where(u < 0.7, tie, np.maximum(tie - 1, 0))))
    else: t = np.where(u < 0.25, tie, moments(rng, uneven, N, R))
    if low is not None: t = np.where(low, rng.integers(0, TM // 2, (N, R)), t)
    M = min(3 * K // 4, 2 * A // (AS + 1))
    hd = np.zeros((N, 8, K), np.int32); vt = moments(rng, uneven, N, 8, V).astype(np.int32); at = moments(rng, uneven, N, 8, A).astype(np.int32)
    vp = rng.integers(0, V + A + 1, (N, 8, V)).astype(np.int32); ap = rng.integers(0, A + 1, (N, 8, A)).astype(np.int32)
    for q in range(N):
        got = own == q; kk, tk, z = key[got], t[got], (q + 1) % N
        for c in range(8):
            x = tt[q, c]; e = np.arange(HS)[:, None] < h[q, c]; no = np.cumsum(e.reshape(-1)).reshape(HS, K) - 1; e = e & (no < V); n = np.sum(e, axis=0)
            ln = rng.integers(1, AS + 1, M)
            if edge: ln = np.where(rng.integers(0, 2, M) > 0, AS, 1); ln[:2] = AS
            e2 = np.arange(AS)[:, None] < ln; no2 = np.cumsum(e2.reshape(-1)).reshape(AS, M) - 1; e2 = e2 & (no2 < A)
            sl, sl2 = rng.permutation(V), rng.permutation(A)
            if edge:
                sl, sl2 = np.arange(V), np.arange(A); sl[1], sl[V - 1] = V - 1, 1; sl2[1], sl2[A - 1] = A - 1, 1
            m = np.where(e2, sl2[np.minimum(no2, A - 1)], A)
            want = np.array([0, 1]) if edge else rng.permutation(kk[low[got]]) if low is not None else np.zeros(0, np.int64)
            p = rng.permutation(K); o = np.concatenate([want, p[~np.isin(p, want)]])[:M]
            cont = np.full(K, A); cont[o] = m[0][np.arange(M) // 2 if share else np.arange(M)]
            ci = ch[q, c][kk]; un = ~np.any((x[ci, :HS] <= tk[:, None]) & (np.arange(HS) < n[ci][:, None]), axis=1)
            w = np.bincount(ci[un], minlength=K); most = U if low is not None else int(rng.integers(U // 2, U + 1)); tot = 0
            for j in o[w[o] > 0].tolist():
                if tot + int(w[j]) <= most: tot += int(w[j])
                else: cont[j] = A
            nx = np.where(e, sl[np.minimum(no, V - 1)], V + cont)
            hd[q, c] = nx[0][ch[q, c]]; vp[q, c][nx[e]] = np.concatenate([nx[1:], (V + cont)[None]])[e]; vt[q, c][nx[e]] = x.T[:HS][e]
            ap[z, c][m[e2]] = np.concatenate([m[1:], np.full((1, M), A)])[e2]; at[z, c][m[e2]] = x[o, HS:].T[e2]
    vv, av = (fine(rng, wide(rng, N, 8, V)), fine(rng, wide(rng, N, 8, A))) if uneven else (fine(rng, f(rng, N, 8, V)), fine(rng, f(rng, N, 8, A)))
    return {"hd": hd, "vt": vt, "vp": vp, "vv": vv, "at": at, "ap": ap, "av": av, "rk": np.stack([table(own[r] * K + key[r]) for r in range(N)]), "rt": np.stack([table(t[r]) for r in range(N)])}
def setup_inputs(rng):
    return make(rng, owners(rng), rng.integers(0, K, (N, R)))
def setup_inputs_caps(rng):
    own = full(rng); key = np.zeros((N, R), np.int64)
    for q in range(N): key[own == q] = rng.permutation(K)[:np.count_nonzero(own == q)]
    far = (own - np.arange(N)[:, None]) % N
    return make(rng, own, key, low=(far == 1) | (far == 2))
def setup_inputs_few(rng):
    own = owners(rng, int(rng.integers(0, N))); pool = np.stack([rng.permutation(K)[:16] for q in range(N)])
    return make(rng, own, pool[own, rng.integers(0, 16, (N, R))])
def setup_inputs_edge(rng):
    pool = np.stack([np.concatenate([np.array([0, 1, K - 1]), 2 + rng.permutation(K - 3)[:29]]) for q in range(N)]); own = owners(rng)
    return make(rng, own, pool[own, rng.integers(0, 32, (N, R))], edge=True)
def setup_inputs_mixed(rng):
    return make(rng, owners(rng), rng.integers(0, K, (N, R)), fall=False, share=True)
def setup_inputs_spread(rng):
    return make(rng, owners(rng), rng.integers(0, K, (N, R)), uneven=True)
def check_inputs(d):
    bad = []
    for a, top in (("hd", V + A + 1), ("vt", TM), ("vp", V + A + 1), ("at", TM), ("ap", A + 1), ("rk", N * K), ("rt", TM)):
        if np.min(d[a]) < 0 or np.max(d[a]) >= top: bad.append(a + "_range")
    for a in ("vv", "av"):
        if not np.isfinite(d[a]).all(): bad.append(a + "_finite")
    if bad: return bad
    hd, vt, vp, n = d["hd"], d["vt"], d["vp"], d["hd"].astype(np.int64); ap = np.roll(d["ap"], -1, axis=0)
    for s in range(HS): n = np.where(n < V, np.take_along_axis(vp, np.minimum(n, V - 1), 2), n)
    if (n < V).any(): bad.append("chain_in_the_heap")
    n = np.maximum(n - V, 0)
    for s in range(AS): n = np.where(n < A, np.take_along_axis(ap, np.minimum(n, A - 1), 2), n)
    if (n < A).any(): bad.append("chain_in_the_archive")
    c = np.arange(8)[:, None]; un = np.zeros((N, 8), np.int64); most = 0
    for r in range(N):
        key, t = entries(d["rk"][r]), entries(d["rt"][r]); q = key // K; most = max(most, int(np.max(np.bincount(q, minlength=N)))); n = hd[q, c, key % K]
        for s in range(HS):
            i = np.minimum(n, V - 1); n = np.where(n < V, np.where(vt[q, c, i] <= t, V + A, vp[q, c, i]), n)
        for g in range(8): un[:, g] += np.bincount(q[(n[g] >= V) & (n[g] < V + A)], minlength=N)
    if most > CAP: bad.append("reads_of_a_pair")
    if np.max(un) > U: bad.append("unfinished_walks")
    return bad
def reference(hd, vt, vp, vv, at, ap, av, rk, rt):
    y = np.zeros((N, 8, R), np.float32); c = np.arange(8)[:, None]
    for r in range(N):
        key, t = entries(rk[r]), entries(rt[r]); q = key // K; z = (q + 1) % N
        n = hd[q, c, key % K]
        for s in range(HS):
            i = np.minimum(n, V - 1); hit = (n < V) & (vt[q, c, i] <= t)
            y[r] = np.where(hit, vv[q, c, i], y[r]); n = np.where(hit, V + A, np.where(n < V, vp[q, c, i], n))
        n = n - V
        for s in range(AS):
            i = np.minimum(n, A - 1); hit = (n < A) & (at[z, c, i] <= t)
            y[r] = np.where(hit, av[z, c, i], y[r]); n = np.where(hit, A, np.where(n < A, ap[z, c, i], n))
    return {"y": y}

@@ -1,0 +1,384 @@
+from concourse.bass import DstId, RemoteDMATransfer
+from concourse.mybir import dt, AluOpType, AxisListType, ActivationFunctionType
+
+N, K, V, A, R = 8, 4096, 8192, 4096, 512
+HW, AW = V + 8, A + 8
+BIG = 2097152.0
+RVP, RVT, RVV, RHD = 0, 1, 2, 3
+COPY = ActivationFunctionType.Copy
+ADD, MUL, MAX, MIN = AluOpType.add, AluOpType.mult, AluOpType.max, AluOpType.min
+GE, GT, LT, EQ = AluOpType.is_ge, AluOpType.is_gt, AluOpType.is_lt, AluOpType.is_equal
+SHR, AND = AluOpType.arith_shift_right, AluOpType.bitwise_and
+
+SCRATCH = {}
+
+
+def declare(where, dtype, **shapes):
+    for n, s in shapes.items():
+        SCRATCH[n] = (where, [128, s], dtype)
+
+
+declare("sbuf", "float32", H=HW, AR=AW, WA=1536, ZF=512, DG=128, C8=32, M32=128, K24=24, PF=8, LB=256, RST=32, OF=4,
+        KF=4, TF=4, O96=4, SC=32, UF=8, LL=512, RR=192, SND=48, RB=48, WW=20, SW=512, X0a=192, X0b=192, XT0=384, TE=48,
+        QM=48, QH=96, MM=48, N4=48, SD2=96, TH=96, QA=96, QB=96, ANS=48, Y0=256, Y1=256)
+declare("sbuf", "int32", RK=4, RT=4, PI=4, OI=4, KI=4, SI=4, UI=8)
+declare("sbuf", "bfloat16", LTI=128, ONE=128, OH=56)
+declare("sbuf", "uint16", U0=4, U1=4, OFW=32, L0=24, LST=48, AL=48)
+declare("psum", "float32", px=512, psc=512, pt=512, pm=512, ph=512, pta=512, pa1=512, pa3=512)
+for _k, _n in (("h", 3), ("a", 4)):
+    for _i in range(1, _n + 1):
+        SCRATCH["X%s%d" % (_k, _i)] = ("sbuf", [128, 776], "float32")
+        for _c in (0, 1):
+            SCRATCH["g%s%d%d" % (_k, _i, _c)] = ("sbuf", [128, 384], "float32")
+            SCRATCH["l%s%d%d" % (_k, _i, _c)] = ("sbuf", [128, 24], "uint16")
+for _n, _s in (("Dhd", [8, K]), ("Dvp", [8, V]), ("Dvt", [8, V]), ("Dap", [8, A]), ("Dat", [8, A]), ("LA", [8, 128, 6])):
+    SCRATCH[_n] = ("dram", _s, "float32")
+SCRATCH["OD"] = ("dram", [2, 128, 4], "uint16")
+TMP = ["M1", "H1", "A1", "H2", "Q2", "PP", "P2", "T3", "H3", "A3", "M3", "B1", "B2", "E2", "N2", "F1", "F2", "F3",
+       "Z2", "B3", "G1", "G2", "Z3", "T4", "B4", "E4"]
+SCRATCH["tmp"] = ("sbuf", [128, 48 * len(TMP)], "float32")
+SEMAPHORES = ["v", "s", "t", "gp", "ldk", "ldt", "chd", "cvp", "cvt", "cap", "cat", "ldh", "lda", "own", "od", "ow",
+              "rB", "lB", "rN", "lN", "rT", "lT", "rF", "lF", "ownf", "wa0", "wa1", "st0", "st1"]
+
+
+def routes(topo, cores, me):
+    src, n = cores[me], len(cores)
+    near, far = [], []
+    for k in range(1, n):
+        d = (me + k) % n
+        (near if topo.chip(cores[d]) == topo.chip(src) else far).append(d)
+    out, used, call, todo = [], [], 0, list(far)
+    if todo:
+        used = list(topo.engines(src, cores[todo[0]]))
+    while todo:
+        m = 1
+        while m * 2 <= min(len(todo), len(used)):
+            m *= 2
+        per = len(used) // m
+        for i in range(m):
+            out.append((todo[i], used[i * per:(i + 1) * per], call))
+        todo = todo[m:]
+        call += 1
+    for d in near:
+        out.append((d, [e for e in topo.engines(src, cores[d]) if e not in used], 0))
+    return out
+
+
+def bits(es):
+    m = 0
+    for e in es:
+        m |= 1 << e
+    return m
+
+
+def rank_program(g, core, T, topo):
+    me = T.rank_of(core)
+    if me is None:
+        return
+    cores = list(T.cores)
+    prv, nxt = (me - 1) % N, (me + 1) % N
+    q = {"v": g.vector, "s": g.scalar, "t": g.tensor, "y": g.sync, "g": g}
+    cnt, seen = {}, {}
+
+    def need(name, toks):
+        for sem, val in toks:
+            if seen.get((name, sem), 0) < val:
+                q[name].wait_ge(T.sem[sem], val)
+                seen[(name, sem)] = val
+
+    def done(ins, sem, n):
+        ins.then_inc(T.sem[sem], n)
+        cnt[sem] = cnt.get(sem, 0) + n
+        return (sem, cnt[sem])
+
+    def tm(name):
+        k = 48 * TMP.index(name)
+        return T.tmp[:, k:k + 48]
+
+    def tt(out, a, b, op, *toks):
+        need("v", toks)
+        return done(g.vector.tensor_tensor(out, a, b, op), "v", 1)
+
+    def ts(out, a, s1, s2, o0, o1, *toks):
+        need("v", toks)
+        if o1 is None:
+            return done(g.vector.tensor_scalar(out, a, s1, None, o0), "v", 1)
+        return done(g.vector.tensor_scalar(out, a, s1, s2, o0, o1), "v", 1)
+
+    def cp(out, a, *toks):
+        need("v", toks)
+        return done(g.vector.tensor_copy(out, a), "v", 1)
+
+    def fill(ap, c, *toks):
+        need("v", toks)
+        return done(g.vector.memset(ap, c), "v", 1)
+
+    def tr(out, a, *toks):
+        need("v", toks)
+        return done(g.vector.transpose(out, a), "v", 1)
+
+    def act(out, a, *toks):
+        need("s", toks)
+        return done(g.scalar.activation(out, a, COPY), "s", 1)
+
+    def mm(out, l, r, start, stop, *toks):
+        need("t", toks)
+        return done(g.tensor.matmul(out, l, r, start, stop), "t", 1)
+
+    def dma(name, out, src, sem, *toks):
+        need(name, toks)
+        return done(q[name].dma_start(out, src), sem, 16)
+
+    def swap(out, src, n, *toks):
+        tk = None
+        for gs in range(2):
+            for G in range(2):
+                k = 256 * gs + 128 * G
+                tk = mm(out[:, gs:n:2], T.SW[:, k:k + 128], src[:, G:n:2], G == 0, G == 1, *toks)
+        return tk
+
+    def iota(out, pat, base, cm, **kw):
+        return done(g.iota(out, pat, base, cm, **kw), "gp", 1)
+
+    fl = {"allow_small_or_imprecise_dtypes": True}
+    k_rk = dma("y", T.RK[:, :], T.rk[:, :], "ldk")
+    k_rt = dma("s", T.RT[:, :], T.rt[:, :], "ldt")
+    i_d = iota(T.DG[:, :], [[1, 128]], 0, -1, **fl)
+    i_c8 = iota(T.C8[:, :], [[0, 4], [1, 8]], 0, 0, **fl)
+    i_pi = iota(T.PI[:, 0:1], [[1, 1]], 0, 1)
+    i_m = iota(T.M32[:, :], [[0, 4], [1, 32]], 0, 0, **fl)
+    i_k = iota(T.K24[:, :], [[1, 24]], 0, 0, **fl)
+    c_hd = dma("g", T.Dhd[:, :], T.hd[:, :], "chd")
+    c_vp = dma("g", T.Dvp[:, :], T.vp[:, :], "cvp")
+    c_vt = dma("g", T.Dvt[:, :], T.vt[:, :], "cvt")
+
+    f0 = fill(T.ZF[:, :], 0.0)
+    fill(T.H[:, V:HW], 8192.0)
+    z1 = fill(T.ONE[:, :], 1.0)
+    z2 = fill(T.OH[:, 0:24], 0.0)
+    ts(T.LB[:, 0:128], T.DG[:, :], 0.0, None, GT, None, i_d)
+    w = ts(T.LB[:, 128:256], T.DG[:, :], 0.0, 1024.0, EQ, MUL)
+    k_lti = tt(T.LTI[:, :], T.LB[:, 0:128], T.LB[:, 128:256], ADD, w)
+    ts(T.RST[:, :], T.C8[:, :], 0.0, None, GT, None, i_c8)
+    ts(T.PI[:, 1:2], T.PI[:, 0:1], 7, None, AND, None, i_pi)
+    w = ts(T.PI[:, 2:3], T.PI[:, 0:1], 4, 1, SHR, AND)
+    w = cp(T.PF[:, 0:2], T.PI[:, 1:3], w)
+    k_bg = ts(T.PF[:, 2:3], T.PF[:, 0:1], float(RVT), BIG, EQ, MUL, w)
+    k_g0 = ts(T.PF[:, 3:4], T.PF[:, 1:2], -1.0, 1.0, MUL, ADD)
+    ts(T.H[:, V:HW], T.H[:, V:HW], T.PF[:, 2:3], None, ADD, None, k_bg)
+    f1 = fill(T.H[:, 0:1536], 0.0)
+    for a0 in range(1536, V, 512):
+        s_hi = act(T.H[:, a0:a0 + 512], T.ZF[:, :], f0)
+        if a0 == 3584:
+            s_lo = s_hi
+
+    w = ts(T.OI[:, :], T.RK[:, :], 12, None, SHR, None, k_rk)
+    k_of = cp(T.OF[:, :], T.OI[:, :], w)
+    for f in range(4):
+        k_oh = ts(T.OH[:, 24 + 8 * f:32 + 8 * f], T.C8[:, 0:8], T.OF[:, f:f + 1], None, EQ, None, k_of, z2)
+    m = mm(T.px[:, 0:32], T.LTI[:, :], T.OH[:, 24:56], True, False, k_lti, k_oh)
+    for d in (1, 2, 3):
+        m = mm(T.px[:, 0:32], T.ONE[:, :], T.OH[:, 24 - 8 * d:56 - 8 * d], False, d == 3, z1)
+    w = ts(T.KI[:, :], T.RK[:, :], 4095, None, AND, None)
+    cp(T.KF[:, :], T.KI[:, :], w)
+    ts(T.TF[:, :], T.RT[:, :], 1.0, None, ADD, None, k_rt)
+    k_o96 = ts(T.O96[:, :], T.OF[:, :], 96.0, -1024.0, MUL, ADD)
+    need("v", [m, k_o96])
+    w = done(g.vector.tensor_tensor_scan(T.SC[:, :], T.RST[:, :], T.px[:, 0:32], 0.0, MUL, MAX), "v", 1)
+    w = tt(T.SI[:, :], T.SC[:, 7:32:8], T.O96[:, :], ADD, w)
+    ts(T.UI[:, 0:4], T.SI[:, :], 31, None, AND, None, w)
+    w = ts(T.UI[:, 4:8], T.SI[:, :], 5, None, SHR, None)
+    k_uf = cp(T.UF[:, :], T.UI[:, :], w)
+    for f in range(4):
+        ts(T.LL[:, 128 * f:128 * f + 128], T.M32[:, :], T.UF[:, f:f + 1], None, EQ, None, k_uf, i_m)
+        ts(T.RR[:, 48 * f:48 * f + 48:2], T.K24[:, :], T.UF[:, 4 + f:5 + f], T.KF[:, f:f + 1], EQ, MUL, i_k)
+        w = ts(T.RR[:, 48 * f + 1:48 * f + 48:2], T.K24[:, :], T.UF[:, 4 + f:5 + f], T.TF[:, f:f + 1], EQ, MUL)
+        m = mm(T.psc[:, 0:48], T.LL[:, 128 * f:128 * f + 128], T.RR[:, 48 * f:48 * f + 48], f == 0, f == 3, w)
+    k_snd = cp(T.SND[:, :], T.psc[:, 0:48], m)
+
+    mine = routes(topo, cores, me)
+
+    def spread(src, dst, rsem, lsem, tok):
+        need("g", [tok])
+        tot = 0
+        for call in range(1 + max(c for _, _, c in mine)):
+            trs = []
+            for d, es, c in mine:
+                if c == call:
+                    rid, pid, _ = topo.addr(cores[d])
+                    trs.append(RemoteDMATransfer(dst_ids=[DstId(rid=rid, pnc=pid)], dma_engine_mask=bits(es), alu_op=0,
+                                                 remote_sem=T.sem[rsem], srcs=[src[:, 6 * d:6 * d + 6]], dsts=[dst]))
+                    tot += len(es)
+            g.remote_dma_fused(trs, local_sem=T.sem[lsem])
+        return (lsem, tot)
+
+    into = sum(len(es) for r in range(N) if r != me for d, es, _ in routes(topo, cores, r) if d == me)
+    l_b = spread(T.SND, T.RB[:, 6 * me:6 * me + 6], "rB", "lB", k_snd)
+    c_ap = dma("g", T.Dap[:, :], T.ap[:, :], "cap")
+    c_at = dma("g", T.Dat[:, :], T["at"][:, :], "cat")
+
+    def rows(win, lo, hi, src, row, sem, *toks):
+        for gam in range(2):
+            for cl in range(2):
+                k = dma("y", win[16 * gam + row + 8 * cl:128:32, lo:hi], src[cl:8:2, lo:hi], sem, *toks)
+        return k
+
+    half = V // 2
+    rows(T.H, 0, half, T.vv, RVV, "ldh", f1, s_lo)
+    rows(T.H, 0, K, T.Dhd, RHD, "ldh", c_hd)
+    rows(T.H, 0, half, T.Dvp, RVP, "ldh", c_vp)
+    rows(T.H, 0, half, T.Dvt, RVT, "ldh", c_vt)
+    k_own = dma("y", T.RB[:, 6 * me:6 * me + 6], T.SND[:, 6 * me:6 * me + 6], "own", k_snd)
+    rows(T.H, half, V, T.vv, RVV, "ldh", s_hi)
+    rows(T.H, half, V, T.Dvp, RVP, "ldh")
+    k_h = rows(T.H, half, V, T.Dvt, RVT, "ldh")
+
+    for gs in range(2):
+        for G in range(2):
+            k = 256 * gs + 128 * G
+            col = T.PF[:, 1:2] if gs else T.PF[:, 3:4]
+            k_sw = ts(T.SW[:, k:k + 128], T.DG[:, :], 16.0 * (G - gs), col, EQ, MUL, k_g0)
+    ts(T.WW[:, 0:4], T.UF[:, 0:4], 6.0, None, MUL, None, k_uf)
+    ts(T.WW[:, 4:8], T.UF[:, 4:8], 2.0, None, MUL, None)
+    w = ts(T.WW[:, 8:12], T.OF[:, :], 186.0, None, MUL, None)
+    w = tt(T.WW[:, 12:16], T.WW[:, 0:4], T.WW[:, 4:8], ADD, w)
+    w = tt(T.WW[:, 16:20], T.WW[:, 12:16], T.WW[:, 8:12], ADD, w)
+    ts(T.U0[:, :], T.WW[:, 16:20], 0.0, None, ADD, None, w)
+    k_u = ts(T.U1[:, :], T.WW[:, 16:20], 1.0, None, ADD, None)
+    w = fill(T.AR[:, A:AW], 4096.0)
+    a_e = ts(T.AR[:, A:AW], T.AR[:, A:AW], T.PF[:, 2:3], None, ADD, None, w)
+    a_f = fill(T.AR[:, 0:2048], 0.0)
+    for b in range(2048, A, 512):
+        a_s = act(T.AR[:, b:b + 512], T.ZF[:, :])
+    for b in range(0, 1536, 512):
+        k_w1 = act(T.WA[:, b:b + 512], T.ZF[:, :])
+
+    dma("y", T.OD[0], T.U0[:, :], "od", k_u)
+    k_od = dma("y", T.OD[1], T.U1[:, :], "od")
+    for gr in range(8):
+        k_ow = dma("y", T.OFW[16 * gr:16 * gr + 16, :], T.OD[gr % 2], "ow", k_od)
+    rows(T.AR, 0, A, T.av, RVV, "lda", a_f, a_s)
+    rows(T.AR, 0, A, T.Dap, RVP, "lda", c_ap)
+    k_ar = rows(T.AR, 0, A, T.Dat, RVT, "lda", c_at)
+
+    def row(x, r, cl=None):
+        a = 8 + r + (384 * cl if cl else 0)
+        return x[:, a:a + (753 if cl is None else 369):16]
+
+    def both(x, cl):
+        return x[:, 24 * cl:24 * cl + 24]
+
+    def hd_row(cl):
+        return T.XT0[:, RHD + 8 * cl:RHD + 8 * cl + 369:16]
+
+    k_l0 = cp(T.L0[:, :], T.RB[:, 0:48:2], ("rB", into), k_own)
+    win = T.H[:, 0:HW]
+    need("v", [k_l0, k_h, s_hi])
+    g0 = done(g.vector.tensor_copy(T.X0a[:, :], win.indirect(T.L0[:, 0:12])), "v", 1)
+    g1 = act(T.X0b[:, :], win.indirect(T.L0[:, 12:24]), k_l0, k_h, s_hi)
+    cp(T.TE[:, 0:24], T.RB[:, 1:48:2])
+    k_te = cp(T.TE[:, 24:48], T.RB[:, 1:48:2])
+    k_pt = swap(T.pt, T.TE, 48, k_te, k_sw)
+    tr(T.XT0[:, 0:192], T.X0a[:, :], g0)
+    w = tr(T.XT0[:, 192:384], T.X0b[:, :], g1)
+    lst = [ts(T["lh1%d" % cl][:, :], hd_row(cl), float(V), None, MIN, None, w) for cl in range(2)]
+    X = {}
+
+    def walk(kind, i, offs, toks, extra, cap, mid=None):
+        x = X[i] = T["X%s%d" % (kind, i)]
+        new, k = [], None
+        for cl in range(2):
+            buf = T["g%s%d%d" % (kind, i, cl)]
+            a = act(buf[:, :], win.indirect(offs[cl]), toks[cl], *extra)
+            o = 384 if cl else 8
+            k = tr(x[:, o:o + 384], buf[:, :], *([a] + ([k] if k else [])))
+            if cap:
+                new.append(ts(T["l%s%d%d" % (kind, i + 1, cl)][:, :], row(x, RVP, cl), cap, None, MIN, None, k))
+            elif mid and not cl:
+                mid()
+        return x, k, new
+
+    def offs(kind, i):
+        return [T["l%s%d%d" % (kind, i, cl)][:, 0:24] for cl in range(2)]
+
+    x, k1, lst = walk("h", 1, offs("h", 1), lst, [k_h], float(V))
+    tt(tm("M1"), row(x, RVT), T.TE[:, :], GE, k1, k_te)
+    w = tt(tm("H1"), row(x, RVT), T.TE[:, :], LT)
+    tt(tm("A1"), tm("H1"), row(x, RVV), MUL, w)
+    x, k2, lst = walk("h", 2, offs("h", 2), lst, [], float(V))
+    for cl in range(2):
+        w = tt(both(T.QM, cl), hd_row(cl), row(x, RVP, cl), MAX, k2)
+    k_pm = swap(T.pm, T.QM, 48, w)
+    tt(T.QH[:, 0:48], row(x, RVT), T.pt[:, 0:48], GE, k_pt)
+    w = tt(tm("H2"), row(x, RVT), T.pt[:, 0:48], LT)
+    w = tt(T.QH[:, 48:96], tm("H2"), row(x, RVV), MUL, w)
+    k_ph = swap(T.ph, T.QH, 96, w)
+    x, k3, lst = walk("h", 3, offs("h", 3), lst, [], None,
+                      lambda: tt(T.MM[:, :], row(X[1], RVP), T.pm[:, 0:48], MAX, k_pm))
+    w = tt(T.N4[:, :], row(x, RVP), T.MM[:, :], MAX, k3)
+    k_n4 = ts(T.LST[:, :], T.N4[:, :], -float(V), None, ADD, None, w)
+
+    zc = cores[nxt]
+    rid, pid, _ = topo.addr(zc)
+    es_d = topo.engines(core, zc)
+    n_in = len(topo.engines(cores[prv], core))
+    need("g", [k_n4])
+    g.remote_dma(T.AL[:, :], T.LST[:, :], T.sem.rN, T.sem.lN, pid, rid, bits(es_d))
+    tt(tm("Q2"), tm("M1"), T.ph[:, 0:48], MUL, k_ph)
+    w = tt(tm("PP"), tm("M1"), T.ph[:, 48:96], MUL)
+    k_t3 = tt(tm("T3"), T.TE[:, :], tm("Q2"), MUL, w)
+    tt(tm("P2"), tm("PP"), tm("A1"), ADD)
+    tt(tm("M3"), row(x, RVT), tm("T3"), GE, k_t3)
+    w = tt(tm("H3"), row(x, RVT), tm("T3"), LT)
+    tt(T.SD2[:, 0:48], tm("T3"), tm("M3"), MUL, w)
+    w = tt(tm("A3"), tm("H3"), row(x, RVV), MUL)
+    k_d2 = tt(T.SD2[:, 48:96], tm("P2"), tm("A3"), ADD, w)
+    need("g", [k_d2])
+    g.remote_dma(T.TH[:, :], T.SD2[:, :], T.sem.rT, T.sem.lT, pid, rid, bits(es_d))
+    r_n, r_t = ("rN", n_in), ("rT", n_in)
+
+    win = T.AR[:, 0:AW]
+    k_pta = swap(T.pta, T.TH, 48, r_t)
+    x, k1, lst = walk("a", 1, [T.AL[:, 0:24], T.AL[:, 24:48]], [r_n, r_n], [k_ar, a_e, a_s], float(A))
+    x, k2, lst = walk("a", 2, offs("a", 2), lst, [], float(A))
+    x1 = X[1]
+    tt(T.QA[:, 0:48], row(x1, RVT), T.pta[:, 0:48], GE, k_pta)
+    w = tt(tm("B1"), row(x1, RVT), T.pta[:, 0:48], LT)
+    w = tt(T.QA[:, 48:96], tm("B1"), row(x1, RVV), MUL, w)
+    k_pa1 = swap(T.pa1, T.QA, 96, w)
+    w = tt(tm("B2"), row(x, RVT), T.TH[:, 0:48], LT, k2, r_t)
+    k_e2 = tt(tm("E2"), tm("B2"), row(x, RVV), MUL, w)
+    x, k3, lst = walk("a", 3, offs("a", 3), lst, [], float(A))
+    tt(T.QB[:, 0:48], row(x, RVT), T.pta[:, 0:48], GE, k3)
+    w = tt(tm("B3"), row(x, RVT), T.pta[:, 0:48], LT)
+    w = tt(T.QB[:, 48:96], tm("B3"), row(x, RVV), MUL, w)
+    k_pa3 = swap(T.pa3, T.QB, 96, w)
+    tt(tm("N2"), row(X[2], RVT), T.TH[:, 0:48], GE)
+    tt(tm("F1"), tm("E2"), T.pa1[:, 0:48], MUL, k_e2, k_pa1)
+    w = tt(tm("F2"), T.TH[:, 48:96], T.pa1[:, 48:96], ADD)
+    tt(tm("F3"), tm("F1"), tm("F2"), ADD, w)
+    k_z2 = tt(tm("Z2"), tm("N2"), T.pa1[:, 0:48], MUL)
+    x, k4, lst = walk("a", 4, offs("a", 4), lst, [], None)
+    tt(tm("Z3"), tm("Z2"), T.pa3[:, 0:48], MUL, k_z2, k_pa3)
+    w = tt(tm("G1"), tm("Z2"), T.pa3[:, 48:96], MUL)
+    tt(tm("T4"), tm("Z3"), T.TH[:, 0:48], MUL, w)
+    w = tt(tm("G2"), tm("G1"), tm("F3"), ADD)
+    w = tt(tm("B4"), row(x, RVT), tm("T4"), LT, w, k4)
+    w = tt(tm("E4"), tm("B4"), row(x, RVV), MUL, w)
+    for cl in range(2):
+        k_ans = tt(T.ANS[:, cl:48:2], both(tm("E4"), cl), both(tm("G2"), cl), ADD, w)
+
+    l_f = spread(T.ANS, T.LA[prv], "rF", "lF", k_ans)
+    k_of2 = dma("y", T.LA[prv], T.ANS[:, 6 * me:6 * me + 6], "ownf", k_ans)
+    ends = []
+    for cl, nm in ((0, "y"), (1, "s")):
+        for a in range(4):
+            p = 32 * a + 16 * cl
+            k = dma(nm, T.WA[p:p + 1, :], T.LA[:, 32 * a:32 * a + 32, :], "wa%d" % cl, ("rF", into), k_of2, k_w1)
+        ends.append(k)
+    need("v", ends + [k_ow])
+    yv = done(g.vector.tensor_copy(T.Y0[:, :], T.WA[:, 0:1536].indirect(T.OFW[:, 0:16])), "v", 1)
+    ys = act(T.Y1[:, :], T.WA[:, 0:1536].indirect(T.OFW[:, 16:32]), *(ends + [k_ow]))
+    dma("y", T.y[:, 0:256], T.Y0[0:128:16, :], "st0", yv)
+    dma("s", T.y[:, 256:512], T.Y1[0:128:16, :], "st1", ys)
+    need("g", [l_b, ("lN", len(es_d)), ("lT", len(es_d)), l_f, r_n, r_t, ("rF", into), ("rB", into)] + list(cnt.items()))

@@ -2,12 +2,13 @@ from concourse.bass import DstId, RemoteDMATransfer
 from concourse.mybir import dt, AluOpType, AxisListType, ActivationFunctionType
 
 N, K, V, A, R = 8, 4096, 8192, 4096, 512
-HW, AW = V + 8, A + 8
+HW = V + 8
 BIG = 2097152.0
 RVP, RVT, RVV, RHD = 0, 1, 2, 3
+ARC, AW = 0, A + 8
 COPY = ActivationFunctionType.Copy
-ADD, MUL, MAX, MIN = AluOpType.add, AluOpType.mult, AluOpType.max, AluOpType.min
-GE, GT, LT, EQ = AluOpType.is_ge, AluOpType.is_gt, AluOpType.is_lt, AluOpType.is_equal
+ADD, SUB, MUL, MAX, MIN = AluOpType.add, AluOpType.subtract, AluOpType.mult, AluOpType.max, AluOpType.min
+GE, GT, LT, EQ, NE = AluOpType.is_ge, AluOpType.is_gt, AluOpType.is_lt, AluOpType.is_equal, AluOpType.not_equal
 SHR, AND = AluOpType.arith_shift_right, AluOpType.bitwise_and
 
 SCRATCH = {}
@@ -18,27 +19,25 @@ def declare(where, dtype, **shapes):
         SCRATCH[n] = (where, [128, s], dtype)
 
 
-declare("sbuf", "float32", H=HW, AR=AW, WA=1536, ZF=512, DG=128, C8=32, M32=128, K24=24, PF=8, LB=256, RST=32, OF=4,
-        KF=4, TF=4, O96=4, SC=32, UF=8, LL=512, RR=192, SND=48, RB=48, WW=20, SW=512, X0a=192, X0b=192, XT0=384, TE=48,
-        QM=48, QH=96, MM=48, N4=48, SD2=96, TH=96, QA=96, QB=96, ANS=48, Y0=256, Y1=256)
-declare("sbuf", "int32", RK=4, RT=4, PI=4, OI=4, KI=4, SI=4, UI=8)
-declare("sbuf", "bfloat16", LTI=128, ONE=128, OH=56)
-declare("sbuf", "uint16", U0=4, U1=4, OFW=32, L0=24, LST=48, AL=48)
-declare("psum", "float32", px=512, psc=512, pt=512, pm=512, ph=512, pta=512, pa1=512, pa3=512)
+declare("sbuf", "float32", H=HW, AR=AW, RA=48, M32=128, RST=32, OF=4, KF=4, TF=4, O96=4, SC=32, UF=8, LL=512, RK2=96, RT2=96,
+        SNT=24, RBT=24, WW=12, SW=512, EYE=128, X0=384, XT0=384, TE=48, QM=48, MM=48, N4=48, SD=96, TH=96, ANS=48,
+        Y0=256, Y1=256, TLF=1792, CF=24, ZF=512)
+declare("sbuf", "int32", RK=4, RT=4, OI=4, KI=4, SI=4, UI=8, TLI=1792)
+declare("sbuf", "bfloat16", ZB=128, LTI=128, ONE=128, OH=56, EYB=128, SWB=512)
+declare("sbuf", "uint16", U0=4, U1=4, OFW=32, SNK=24, L0=24, LST0=24, LST1=24, AL0=24, AL1=24)
+declare("psum", "float32", p0=512, p1=512, p2=512, p3=512, p4=512, p5=512, p6=512, p7=512)
 for _k, _n in (("h", 3), ("a", 4)):
     for _i in range(1, _n + 1):
         SCRATCH["X%s%d" % (_k, _i)] = ("sbuf", [128, 776], "float32")
+        SCRATCH["h%s%d" % (_k, _i)] = ("sbuf", [128, 48], "bfloat16")
+        SCRATCH["e%s%d" % (_k, _i)] = ("sbuf", [128, 48], "float32")
         for _c in (0, 1):
             SCRATCH["g%s%d%d" % (_k, _i, _c)] = ("sbuf", [128, 384], "float32")
-            SCRATCH["l%s%d%d" % (_k, _i, _c)] = ("sbuf", [128, 24], "uint16")
-for _n, _s in (("Dhd", [8, K]), ("Dvp", [8, V]), ("Dvt", [8, V]), ("Dap", [8, A]), ("Dat", [8, A]), ("LA", [8, 128, 6])):
-    SCRATCH[_n] = ("dram", _s, "float32")
+            if _k == "h" or _i > 1:
+                SCRATCH["l%s%d%d" % (_k, _i, _c)] = ("sbuf", [128, 24], "uint16")
 SCRATCH["OD"] = ("dram", [2, 128, 4], "uint16")
-TMP = ["M1", "H1", "A1", "H2", "Q2", "PP", "P2", "T3", "H3", "A3", "M3", "B1", "B2", "E2", "N2", "F1", "F2", "F3",
-       "Z2", "B3", "G1", "G2", "Z3", "T4", "B4", "E4"]
-SCRATCH["tmp"] = ("sbuf", [128, 48 * len(TMP)], "float32")
-SEMAPHORES = ["v", "s", "t", "gp", "ldk", "ldt", "chd", "cvp", "cvt", "cap", "cat", "ldh", "lda", "own", "od", "ow",
-              "rB", "lB", "rN", "lN", "rT", "lT", "rF", "lF", "ownf", "wa0", "wa1", "st0", "st1"]
+SEMAPHORES = ["v", "s", "t", "gp", "ldk", "ldt", "thd", "tvp", "tvt", "tar", "ldh", "ldi", "lda", "ownk", "ownt", "od", "ow",
+              "rK", "rB", "lB", "rN0", "rN1", "rT", "rF", "ownf", "wa0", "wa1", "st0", "st1"]
 
 
 def routes(topo, cores, me):
@@ -60,7 +59,7 @@ def routes(topo, cores, me):
         todo = todo[m:]
         call += 1
     for d in near:
-        out.append((d, [e for e in topo.engines(src, cores[d]) if e not in used], 0))
+        out.append((d, [e for e in topo.engines(src, cores[d]) if e not in used][:2], 0))
     return out
 
 
@@ -90,10 +89,6 @@ def rank_program(g, core, T, topo):
         ins.then_inc(T.sem[sem], n)
         cnt[sem] = cnt.get(sem, 0) + n
         return (sem, cnt[sem])
-
-    def tm(name):
-        k = 48 * TMP.index(name)
-        return T.tmp[:, k:k + 48]
 
     def tt(out, a, b, op, *toks):
         need("v", toks)
@@ -129,137 +124,168 @@ def rank_program(g, core, T, topo):
         need(name, toks)
         return done(q[name].dma_start(out, src), sem, 16)
 
-    def swap(out, src, n, *toks):
+    def swap(out, src, mat, start, stop, *toks):
         tk = None
         for gs in range(2):
             for G in range(2):
                 k = 256 * gs + 128 * G
-                tk = mm(out[:, gs:n:2], T.SW[:, k:k + 128], src[:, G:n:2], G == 0, G == 1, *toks)
+                tk = mm(out[:, gs:48:2], mat[:, k:k + 128], src[:, G:48:2], start and gs + G == 0, stop and gs + G == 2,
+                        *toks)
         return tk
 
     def iota(out, pat, base, cm, **kw):
         return done(g.iota(out, pat, base, cm, **kw), "gp", 1)
 
+    def pick(out, zero, pat, op, val, base, cm, *toks):
+        need("g", toks)
+        return done(g.affine_select(out, zero, pat, op, val, base, cm), "gp", 1)
+
     fl = {"allow_small_or_imprecise_dtypes": True}
     k_rk = dma("y", T.RK[:, :], T.rk[:, :], "ldk")
     k_rt = dma("s", T.RT[:, :], T.rt[:, :], "ldt")
-    i_d = iota(T.DG[:, :], [[1, 128]], 0, -1, **fl)
-    i_c8 = iota(T.C8[:, :], [[0, 4], [1, 8]], 0, 0, **fl)
-    i_pi = iota(T.PI[:, 0:1], [[1, 1]], 0, 1)
-    i_m = iota(T.M32[:, :], [[0, 4], [1, 32]], 0, 0, **fl)
-    i_k = iota(T.K24[:, :], [[1, 24]], 0, 0, **fl)
-    c_hd = dma("g", T.Dhd[:, :], T.hd[:, :], "chd")
-    c_vp = dma("g", T.Dvp[:, :], T.vp[:, :], "cvp")
-    c_vt = dma("g", T.Dvt[:, :], T.vt[:, :], "cvt")
+    tiles = {"hd": (0, 1), "vp": (256, 2), "vt": (768, 2), "ap": (1280, 1), "at": (1536, 1)}
 
+    def tile(buf, name, piece, cl):
+        c0, n = tiles[name]
+        p0, h = 64 // n * (2 * piece + cl), 64 // n
+        return buf[p0:p0 + h, c0:c0 + 256 * n]
+
+    k_tl = {}
+    for name, sem in (("hd", "thd"), ("vp", "tvp"), ("vt", "tvt"), ("ap", "tar"), ("at", "tar")):
+        for piece in range(tiles[name][1]):
+            for cl in range(2):
+                k_tl[name] = dma("y", tile(T.TLI, name, piece, cl), T[name][cl:8:2, A * piece:A * piece + A], sem)
+    z0 = fill(T.ZB[:, :], 0.0)
     f0 = fill(T.ZF[:, :], 0.0)
-    fill(T.H[:, V:HW], 8192.0)
+    i_m = iota(T.M32[:, :], [[0, 4], [1, 32]], 0, 0, **fl)
+    pick(T.LTI[:, :], T.ZB[:, :], [[-1, 128]], GE, 1.0, 0, 1, z0)
+    k_lti = pick(T.EYB[:, :], T.ZB[:, :], [[1, 128]], NE, -BIG, 0, -1)
+    G0, V0, V1 = 3072, 768, 6144
+    i_h = iota(T.H[:, G0:K], [[0, K - G0]], 0, 0, **fl)
+
     z1 = fill(T.ONE[:, :], 1.0)
     z2 = fill(T.OH[:, 0:24], 0.0)
-    ts(T.LB[:, 0:128], T.DG[:, :], 0.0, None, GT, None, i_d)
-    w = ts(T.LB[:, 128:256], T.DG[:, :], 0.0, 1024.0, EQ, MUL)
-    k_lti = tt(T.LTI[:, :], T.LB[:, 0:128], T.LB[:, 128:256], ADD, w)
-    ts(T.RST[:, :], T.C8[:, :], 0.0, None, GT, None, i_c8)
-    ts(T.PI[:, 1:2], T.PI[:, 0:1], 7, None, AND, None, i_pi)
-    w = ts(T.PI[:, 2:3], T.PI[:, 0:1], 4, 1, SHR, AND)
-    w = cp(T.PF[:, 0:2], T.PI[:, 1:3], w)
-    k_bg = ts(T.PF[:, 2:3], T.PF[:, 0:1], float(RVT), BIG, EQ, MUL, w)
-    k_g0 = ts(T.PF[:, 3:4], T.PF[:, 1:2], -1.0, 1.0, MUL, ADD)
-    ts(T.H[:, V:HW], T.H[:, V:HW], T.PF[:, 2:3], None, ADD, None, k_bg)
-    f1 = fill(T.H[:, 0:1536], 0.0)
-    for a0 in range(1536, V, 512):
-        s_hi = act(T.H[:, a0:a0 + 512], T.ZF[:, :], f0)
-        if a0 == 3584:
-            s_lo = s_hi
+    w = fill(T.RST[:, :], 1.0)
+    f1 = fill(T.H[:, 0:V0], 0.0)
+    fill(T.RST[:, 0:32:8], 0.0, w)
+
+    def sfill(lo, hi, *toks):
+        for a0 in range(lo, hi, 512):
+            n = min(512, hi - a0)
+            k = act(T.H[:, a0:a0 + n], T.ZF[:, 0:n], *toks)
+        return k
+
+    def convert(name):
+        c0, n = tiles[name]
+        return act(T.TLF[:, c0:c0 + 256 * n], T.TLI[:, c0:c0 + 256 * n], k_tl[name])
+
+    s_1 = sfill(V0, 2048, f0)
+    c_hd = convert("hd")
+    sfill(2048, 2560)
+    c_vp = convert("vp")
+    s_2 = sfill(2560, G0)
+    c_vt = convert("vt")
+    s_3 = sfill(K, V1)
 
     w = ts(T.OI[:, :], T.RK[:, :], 12, None, SHR, None, k_rk)
     k_of = cp(T.OF[:, :], T.OI[:, :], w)
     for f in range(4):
-        k_oh = ts(T.OH[:, 24 + 8 * f:32 + 8 * f], T.C8[:, 0:8], T.OF[:, f:f + 1], None, EQ, None, k_of, z2)
-    m = mm(T.px[:, 0:32], T.LTI[:, :], T.OH[:, 24:56], True, False, k_lti, k_oh)
+        k_oh = ts(T.OH[:, 24 + 8 * f:32 + 8 * f], T.M32[:, 0:8], T.OF[:, f:f + 1], None, EQ, None, k_of, z2, i_m)
+    mm(T.p0[:, 0:32], T.LTI[:, :], T.OH[:, 24:56], True, False, k_lti, k_oh)
+    mm(T.p0[:, 0:32], T.EYB[:, :], T.OH[:, 24:56], False, False)
     for d in (1, 2, 3):
-        m = mm(T.px[:, 0:32], T.ONE[:, :], T.OH[:, 24 - 8 * d:56 - 8 * d], False, d == 3, z1)
+        m = mm(T.p0[:, 0:32], T.ONE[:, :], T.OH[:, 24 - 8 * d:56 - 8 * d], False, d == 3, z1)
     w = ts(T.KI[:, :], T.RK[:, :], 4095, None, AND, None)
-    cp(T.KF[:, :], T.KI[:, :], w)
-    ts(T.TF[:, :], T.RT[:, :], 1.0, None, ADD, None, k_rt)
-    k_o96 = ts(T.O96[:, :], T.OF[:, :], 96.0, -1024.0, MUL, ADD)
+    k_o96 = ts(T.O96[:, :], T.OF[:, :], 96.0, BIG, MUL, ADD)
+    k_kf = cp(T.KF[:, :], T.KI[:, :], w)
     need("v", [m, k_o96])
-    w = done(g.vector.tensor_tensor_scan(T.SC[:, :], T.RST[:, :], T.px[:, 0:32], 0.0, MUL, MAX), "v", 1)
+    w = done(g.vector.tensor_tensor_scan(T.SC[:, :], T.RST[:, :], T.p0[:, 0:32], 0.0, MUL, MIN), "v", 1)
     w = tt(T.SI[:, :], T.SC[:, 7:32:8], T.O96[:, :], ADD, w)
     ts(T.UI[:, 0:4], T.SI[:, :], 31, None, AND, None, w)
     w = ts(T.UI[:, 4:8], T.SI[:, :], 5, None, SHR, None)
     k_uf = cp(T.UF[:, :], T.UI[:, :], w)
     for f in range(4):
-        ts(T.LL[:, 128 * f:128 * f + 128], T.M32[:, :], T.UF[:, f:f + 1], None, EQ, None, k_uf, i_m)
-        ts(T.RR[:, 48 * f:48 * f + 48:2], T.K24[:, :], T.UF[:, 4 + f:5 + f], T.KF[:, f:f + 1], EQ, MUL, i_k)
-        w = ts(T.RR[:, 48 * f + 1:48 * f + 48:2], T.K24[:, :], T.UF[:, 4 + f:5 + f], T.TF[:, f:f + 1], EQ, MUL)
-        m = mm(T.psc[:, 0:48], T.LL[:, 128 * f:128 * f + 128], T.RR[:, 48 * f:48 * f + 48], f == 0, f == 3, w)
-    k_snd = cp(T.SND[:, :], T.psc[:, 0:48], m)
+        ts(T.RK2[:, 24 * f:24 * f + 24], T.M32[:, 0:24], T.UF[:, 4 + f:5 + f], T.KF[:, f:f + 1], EQ, MUL, k_uf)
+        w = ts(T.LL[:, 128 * f:128 * f + 128], T.M32[:, :], T.UF[:, f:f + 1], None, EQ, None)
+        m = mm(T.p1[:, 0:24], T.LL[:, 128 * f:128 * f + 128], T.RK2[:, 24 * f:24 * f + 24], f == 0, f == 3, w)
+    k_tf = ts(T.TF[:, :], T.RT[:, :], 1.0, None, ADD, None, k_rt)
+    k_snk = cp(T.SNK[:, :], T.p1[:, 0:24], m)
+    for f in range(4):
+        w = ts(T.RT2[:, 24 * f:24 * f + 24], T.M32[:, 0:24], T.UF[:, 4 + f:5 + f], T.TF[:, f:f + 1], EQ, MUL, k_tf)
+        m = mm(T.p2[:, 0:24], T.LL[:, 128 * f:128 * f + 128], T.RT2[:, 24 * f:24 * f + 24], f == 0, f == 3, w)
+    fill(T.H[:, V1:V1 + 512], 0.0)
+    k_snt = cp(T.SNT[:, :], T.p2[:, 0:24], m)
+    fill(T.CF[:, 0:8], float(V))
+    fill(T.CF[:, 8:16], float(A))
+    fill(T.CF[:, 16:24], BIG)
+    fill(T.AR[:, A:AW], 0.0)
+    f2 = fill(T.H[:, V1 + 512:HW], 0.0)
+    c_ar = cp(T.TLF[:, 1280:1792], T.TLI[:, 1280:1792], k_tl["at"])
 
     mine = routes(topo, cores, me)
+    sent = [0]
 
-    def spread(src, dst, rsem, lsem, tok):
+    def spread(src, n, dst, rsem, tok):
         need("g", [tok])
-        tot = 0
         for call in range(1 + max(c for _, _, c in mine)):
             trs = []
             for d, es, c in mine:
                 if c == call:
                     rid, pid, _ = topo.addr(cores[d])
                     trs.append(RemoteDMATransfer(dst_ids=[DstId(rid=rid, pnc=pid)], dma_engine_mask=bits(es), alu_op=0,
-                                                 remote_sem=T.sem[rsem], srcs=[src[:, 6 * d:6 * d + 6]], dsts=[dst]))
-                    tot += len(es)
-            g.remote_dma_fused(trs, local_sem=T.sem[lsem])
-        return (lsem, tot)
+                                                 remote_sem=T.sem[rsem], srcs=[src[:, n * d:n * d + n]], dsts=[dst]))
+                    sent[0] += len(es)
+            g.remote_dma_fused(trs, local_sem=T.sem.lB)
 
     into = sum(len(es) for r in range(N) if r != me for d, es, _ in routes(topo, cores, r) if d == me)
-    l_b = spread(T.SND, T.RB[:, 6 * me:6 * me + 6], "rB", "lB", k_snd)
-    c_ap = dma("g", T.Dap[:, :], T.ap[:, :], "cap")
-    c_at = dma("g", T.Dat[:, :], T["at"][:, :], "cat")
+    spread(T.SNK, 3, T.L0[:, 3 * me:3 * me + 3], "rK", k_snk)
+    spread(T.SNT, 3, T.RBT[:, 3 * me:3 * me + 3], "rB", k_snt)
 
-    def rows(win, lo, hi, src, row, sem, *toks):
+    k_eye = pick(T.EYE[:, :], T.ZF[:, 0:128], [[1, 128]], NE, 1.0, 0, -1, f0)
+    for mat, zero, val in ((T.SW, T.ZF, 1.0), (T.SWB, T.ZB, -BIG)):
+        for gs in range(2):
+            for G in range(2):
+                k = 256 * gs + 128 * G
+                k_swb = pick(mat[:, k:k + 128], zero[:, 0:128], [[32, 4], [1016, 2], [1, 16]], NE, val,
+                             -1000 * G - 16 * (G - gs), -1)
+        if val > 0:
+            k_sw = k_swb
+
+    def rows(lo, hi, src, row, sem, *toks):
         for gam in range(2):
             for cl in range(2):
-                k = dma("y", win[16 * gam + row + 8 * cl:128:32, lo:hi], src[cl:8:2, lo:hi], sem, *toks)
+                k = dma("y", win[16 * gam + row + 8 * cl:128:32, lo:hi], src(cl), sem, *toks)
         return k
 
-    half = V // 2
-    rows(T.H, 0, half, T.vv, RVV, "ldh", f1, s_lo)
-    rows(T.H, 0, K, T.Dhd, RHD, "ldh", c_hd)
-    rows(T.H, 0, half, T.Dvp, RVP, "ldh", c_vp)
-    rows(T.H, 0, half, T.Dvt, RVT, "ldh", c_vt)
-    k_own = dma("y", T.RB[:, 6 * me:6 * me + 6], T.SND[:, 6 * me:6 * me + 6], "own", k_snd)
-    rows(T.H, half, V, T.vv, RVV, "ldh", s_hi)
-    rows(T.H, half, V, T.Dvp, RVP, "ldh")
-    k_h = rows(T.H, half, V, T.Dvt, RVT, "ldh")
+    win = T.H
 
-    for gs in range(2):
-        for G in range(2):
-            k = 256 * gs + 128 * G
-            col = T.PF[:, 1:2] if gs else T.PF[:, 3:4]
-            k_sw = ts(T.SW[:, k:k + 128], T.DG[:, :], 16.0 * (G - gs), col, EQ, MUL, k_g0)
-    ts(T.WW[:, 0:4], T.UF[:, 0:4], 6.0, None, MUL, None, k_uf)
-    ts(T.WW[:, 4:8], T.UF[:, 4:8], 2.0, None, MUL, None)
-    w = ts(T.WW[:, 8:12], T.OF[:, :], 186.0, None, MUL, None)
-    w = tt(T.WW[:, 12:16], T.WW[:, 0:4], T.WW[:, 4:8], ADD, w)
-    w = tt(T.WW[:, 16:20], T.WW[:, 12:16], T.WW[:, 8:12], ADD, w)
-    ts(T.U0[:, :], T.WW[:, 16:20], 0.0, None, ADD, None, w)
-    k_u = ts(T.U1[:, :], T.WW[:, 16:20], 1.0, None, ADD, None)
-    w = fill(T.AR[:, A:AW], 4096.0)
-    a_e = ts(T.AR[:, A:AW], T.AR[:, A:AW], T.PF[:, 2:3], None, ADD, None, w)
-    a_f = fill(T.AR[:, 0:2048], 0.0)
-    for b in range(2048, A, 512):
-        a_s = act(T.AR[:, b:b + 512], T.ZF[:, :])
-    for b in range(0, 1536, 512):
-        k_w1 = act(T.WA[:, b:b + 512], T.ZF[:, :])
+    def cols(t, lo, hi):
+        return lambda cl: t[cl:8:2, lo:hi]
 
-    dma("y", T.OD[0], T.U0[:, :], "od", k_u)
-    k_od = dma("y", T.OD[1], T.U1[:, :], "od")
-    for gr in range(8):
-        k_ow = dma("y", T.OFW[16 * gr:16 * gr + 16, :], T.OD[gr % 2], "ow", k_od)
-    rows(T.AR, 0, A, T.av, RVV, "lda", a_f, a_s)
-    rows(T.AR, 0, A, T.Dap, RVP, "lda", c_ap)
-    k_ar = rows(T.AR, 0, A, T.Dat, RVT, "lda", c_at)
+    def conv(name, piece):
+        return lambda cl: tile(T.TLF, name, piece, cl)
+
+    rows(0, 2048, cols(T.vv, 0, 2048), RVV, "ldh", f1, s_1)
+    rows(2048, K, cols(T.vv, 2048, K), RVV, "ldh", s_2, i_h)
+    rows(0, K, conv("hd", 0), RHD, "ldh", c_hd)
+    rows(0, K, conv("vp", 0), RVP, "ldh", c_vp)
+    k_h0 = rows(0, K, conv("vt", 0), RVT, "ldh", c_vt)
+    k_own = dma("y", T.L0[:, 3 * me:3 * me + 3], T.SNK[:, 3 * me:3 * me + 3], "ownk", k_snk)
+    rows(K, V1, cols(T.vv, K, V1), RVV, "ldi", s_3)
+    rows(K, V, conv("vp", 1), RVP, "ldi", f2)
+    rows(K, V, conv("vt", 1), RVT, "ldi")
+    rows(V1, V, cols(T.vv, V1, V), RVV, "ldi")
+    dma("y", T.H[RVP:128:8, V:HW], T.CF[0:16, 0:8], "ldi")
+    k_h = dma("y", T.H[RVT:128:8, V:HW], T.CF[0:16, 16:24], "ldi")
+    k_ownt = dma("y", T.RBT[:, 3 * me:3 * me + 3], T.SNT[:, 3 * me:3 * me + 3], "ownt", k_snt)
+    win = T.AR
+    rows(0, A, cols(T.av, 0, A), RVV, "lda")
+    rows(0, A, conv("ap", 0), RVP, "lda", c_ar)
+    rows(0, A, conv("at", 0), RVT, "lda")
+    for r in range(RVV + 1, 8):
+        dma("y", T.AR[r:128:8, 0:A], T.vv[:, :], "lda")
+    dma("y", T.AR[RVP:128:8, A:AW], T.CF[0:16, 8:16], "lda")
+    k_ar = dma("y", T.AR[RVT:128:8, A:AW], T.CF[0:16, 16:24], "lda")
 
     def row(x, r, cl=None):
         a = 8 + r + (384 * cl if cl else 0)
@@ -271,20 +297,15 @@ def rank_program(g, core, T, topo):
     def hd_row(cl):
         return T.XT0[:, RHD + 8 * cl:RHD + 8 * cl + 369:16]
 
-    k_l0 = cp(T.L0[:, :], T.RB[:, 0:48:2], ("rB", into), k_own)
-    win = T.H[:, 0:HW]
-    need("v", [k_l0, k_h, s_hi])
-    g0 = done(g.vector.tensor_copy(T.X0a[:, :], win.indirect(T.L0[:, 0:12])), "v", 1)
-    g1 = act(T.X0b[:, :], win.indirect(T.L0[:, 12:24]), k_l0, k_h, s_hi)
-    cp(T.TE[:, 0:24], T.RB[:, 1:48:2])
-    k_te = cp(T.TE[:, 24:48], T.RB[:, 1:48:2])
-    k_pt = swap(T.pt, T.TE, 48, k_te, k_sw)
-    tr(T.XT0[:, 0:192], T.X0a[:, :], g0)
-    w = tr(T.XT0[:, 192:384], T.X0b[:, :], g1)
+    r_k = ("rK", into)
+    need("v", [r_k, k_own, k_h0])
+    g0 = done(g.vector.tensor_copy(T.X0[:, 0:192], T.H[:, 0:K].indirect(T.L0[:, 0:12])), "v", 1)
+    g1 = act(T.X0[:, 192:384], T.H[:, 0:K].indirect(T.L0[:, 12:24]), r_k, k_own, k_h0)
+    w = tr(T.XT0[:, :], T.X0[:, :], g0, g1)
     lst = [ts(T["lh1%d" % cl][:, :], hd_row(cl), float(V), None, MIN, None, w) for cl in range(2)]
-    X = {}
+    X, first = {}, {"h": 0, "a": ARC}
 
-    def walk(kind, i, offs, toks, extra, cap, mid=None):
+    def walk(kind, i, win, offs, toks, extra, after):
         x = X[i] = T["X%s%d" % (kind, i)]
         new, k = [], None
         for cl in range(2):
@@ -292,93 +313,137 @@ def rank_program(g, core, T, topo):
             a = act(buf[:, :], win.indirect(offs[cl]), toks[cl], *extra)
             o = 384 if cl else 8
             k = tr(x[:, o:o + 384], buf[:, :], *([a] + ([k] if k else [])))
-            if cap:
-                new.append(ts(T["l%s%d%d" % (kind, i + 1, cl)][:, :], row(x, RVP, cl), cap, None, MIN, None, k))
-            elif mid and not cl:
-                mid()
-        return x, k, new
+            new.append(after(cl, x, k))
+        return new
 
     def offs(kind, i):
         return [T["l%s%d%d" % (kind, i, cl)][:, 0:24] for cl in range(2)]
 
-    x, k1, lst = walk("h", 1, offs("h", 1), lst, [k_h], float(V))
-    tt(tm("M1"), row(x, RVT), T.TE[:, :], GE, k1, k_te)
-    w = tt(tm("H1"), row(x, RVT), T.TE[:, :], LT)
-    tt(tm("A1"), tm("H1"), row(x, RVV), MUL, w)
-    x, k2, lst = walk("h", 2, offs("h", 2), lst, [], float(V))
-    for cl in range(2):
-        w = tt(both(T.QM, cl), hd_row(cl), row(x, RVP, cl), MAX, k2)
-    k_pm = swap(T.pm, T.QM, 48, w)
-    tt(T.QH[:, 0:48], row(x, RVT), T.pt[:, 0:48], GE, k_pt)
-    w = tt(tm("H2"), row(x, RVT), T.pt[:, 0:48], LT)
-    w = tt(T.QH[:, 48:96], tm("H2"), row(x, RVV), MUL, w)
-    k_ph = swap(T.ph, T.QH, 96, w)
-    x, k3, lst = walk("h", 3, offs("h", 3), lst, [], None,
-                      lambda: tt(T.MM[:, :], row(X[1], RVP), T.pm[:, 0:48], MAX, k_pm))
-    w = tt(T.N4[:, :], row(x, RVP), T.MM[:, :], MAX, k3)
-    k_n4 = ts(T.LST[:, :], T.N4[:, :], -float(V), None, ADD, None, w)
+    def nextlist(kind, i, cl, x, k, cap):
+        return ts(T["l%s%d%d" % (kind, i + 1, cl)][:, :], row(x, first[kind] + RVP, cl), cap, None, MIN, None, k)
+
+    def compare(kind, i, open_t, *toks):
+        h, e = T["h%s%d" % (kind, i)], T["e%s%d" % (kind, i)]
+        kh = tt(h[:, :], row(X[i], first[kind] + RVT), open_t, LT, *toks)
+        return kh, tt(e[:, :], h[:, :], row(X[i], first[kind] + RVV), MUL, kh)
+
+    S = {}
+    win = T.H[:, 0:HW]
+
+    def heap1(cl, x, k):
+        new = nextlist("h", 1, cl, x, k, float(V))
+        if cl == 0:
+            cp(T.TE[:, 0:24], T.RBT[:, :], ("rB", into), k_ownt)
+            S["te"] = cp(T.TE[:, 24:48], T.RBT[:, :])
+            swap(T.p1, T.TE, T.SW, True, False, S["te"], k_sw)
+            mm(T.p2[:, 0:48], T.EYE[:, :], T.TE[:, :], True, False, k_eye)
+            mm(T.p3[:, 0:48], T.EYE[:, :], T.TE[:, :], True, False)
+        else:
+            kh, ke = compare("h", 1, T.TE[:, :], S["te"], k)
+            S["t2"] = swap(T.p1, T.hh1, T.SWB, False, True, kh, k_swb)
+            mm(T.p2[:, 0:48], T.EYB[:, :], T.hh1[:, :], False, False)
+            mm(T.p3[:, 0:48], T.EYB[:, :], T.hh1[:, :], False, False)
+            mm(T.p4[:, 0:48], T.EYE[:, :], T.eh1[:, :], True, False, ke)
+        return new
+
+    def heap2(cl, x, k):
+        new = nextlist("h", 2, cl, x, k, float(V))
+        w = tt(both(T.QM, cl), hd_row(cl), row(x, RVP, cl), MAX)
+        if cl == 1:
+            S["pm"] = swap(T.p5, T.QM, T.SW, True, True, w)
+            kh, ke = compare("h", 2, T.p1[:, 0:48], S["t2"])
+            S["t3"] = swap(T.p2, T.hh2, T.SWB, False, True, kh)
+            swap(T.p3, T.hh2, T.SWB, False, False)
+            S["v2"] = swap(T.p4, T.eh2, T.SW, False, True, ke)
+        return new
 
     zc = cores[nxt]
     rid, pid, _ = topo.addr(zc)
-    es_d = topo.engines(core, zc)
-    n_in = len(topo.engines(cores[prv], core))
-    need("g", [k_n4])
-    g.remote_dma(T.AL[:, :], T.LST[:, :], T.sem.rN, T.sem.lN, pid, rid, bits(es_d))
-    tt(tm("Q2"), tm("M1"), T.ph[:, 0:48], MUL, k_ph)
-    w = tt(tm("PP"), tm("M1"), T.ph[:, 48:96], MUL)
-    k_t3 = tt(tm("T3"), T.TE[:, :], tm("Q2"), MUL, w)
-    tt(tm("P2"), tm("PP"), tm("A1"), ADD)
-    tt(tm("M3"), row(x, RVT), tm("T3"), GE, k_t3)
-    w = tt(tm("H3"), row(x, RVT), tm("T3"), LT)
-    tt(T.SD2[:, 0:48], tm("T3"), tm("M3"), MUL, w)
-    w = tt(tm("A3"), tm("H3"), row(x, RVV), MUL)
-    k_d2 = tt(T.SD2[:, 48:96], tm("P2"), tm("A3"), ADD, w)
-    need("g", [k_d2])
-    g.remote_dma(T.TH[:, :], T.SD2[:, :], T.sem.rT, T.sem.lT, pid, rid, bits(es_d))
-    r_n, r_t = ("rN", n_in), ("rT", n_in)
+    far_n = min(len(topo.engines(cores[r], cores[(r + 1) % N])) for r in range(N))
+    es_d = topo.engines(core, zc)[:far_n]
+
+    def onward(dst, src, rsem, tok):
+        need("g", [tok])
+        g.remote_dma(dst, src, T.sem[rsem], T.sem.lB, pid, rid, bits(es_d))
+        sent[0] += far_n
+        return (rsem, far_n)
+
+    def heap3(cl, x, k):
+        if cl == 0:
+            S["mm"] = tt(T.MM[:, :], row(X[1], RVP), T.p5[:, 0:48], MAX, S["pm"])
+        w = tt(both(T.N4, cl), row(x, RVP, cl), both(T.MM, cl), MAX, k, S["mm"])
+        w = ts(T["LST%d" % cl][:, :], both(T.N4, cl), -float(V), None, ADD, None, w)
+        return onward(T["AL%d" % cl][:, :], T["LST%d" % cl][:, :], "rN%d" % cl, w)
+
+    lst = walk("h", 1, win, offs("h", 1), lst, [k_h], heap1)
+    lst = walk("h", 2, win, offs("h", 2), lst, [], heap2)
+    r_n = walk("h", 3, win, offs("h", 3), lst, [], heap3)
+    kh, ke = compare("h", 3, T.p2[:, 0:48], S["t3"])
+    k_t4 = mm(T.p3[:, 0:48], T.EYB[:, :], T.hh3[:, :], False, True, kh)
+    tt(T.SD[:, 48:96], T.eh3[:, :], T.p4[:, 0:48], ADD, ke, S["v2"])
+    w = cp(T.SD[:, 0:48], T.p3[:, 0:48], k_t4)
+    r_t = onward(T.TH[:, :], T.SD[:, :], "rT", w)
+    ts(T.WW[:, 0:4], T.UF[:, 0:4], 48.0, None, MUL, None)
+    w = ts(T.WW[:, 4:8], T.UF[:, 4:8], 2.0, None, MUL, None)
+    w = tt(T.WW[:, 8:12], T.WW[:, 0:4], T.WW[:, 4:8], ADD, w)
+    ts(T.U0[:, :], T.WW[:, 8:12], 0.0, None, ADD, None, w)
+    k_u = ts(T.U1[:, :], T.WW[:, 8:12], 1.0, None, ADD, None)
+    dma("y", T.OD[0], T.U0[:, :], "od", k_u)
+    k_od = dma("y", T.OD[1], T.U1[:, :], "od")
+    for gr in range(8):
+        k_ow = dma("y", T.OFW[16 * gr:16 * gr + 16, :], T.OD[gr % 2], "ow", k_od)
 
     win = T.AR[:, 0:AW]
-    k_pta = swap(T.pta, T.TH, 48, r_t)
-    x, k1, lst = walk("a", 1, [T.AL[:, 0:24], T.AL[:, 24:48]], [r_n, r_n], [k_ar, a_e, a_s], float(A))
-    x, k2, lst = walk("a", 2, offs("a", 2), lst, [], float(A))
-    x1 = X[1]
-    tt(T.QA[:, 0:48], row(x1, RVT), T.pta[:, 0:48], GE, k_pta)
-    w = tt(tm("B1"), row(x1, RVT), T.pta[:, 0:48], LT)
-    w = tt(T.QA[:, 48:96], tm("B1"), row(x1, RVV), MUL, w)
-    k_pa1 = swap(T.pa1, T.QA, 96, w)
-    w = tt(tm("B2"), row(x, RVT), T.TH[:, 0:48], LT, k2, r_t)
-    k_e2 = tt(tm("E2"), tm("B2"), row(x, RVV), MUL, w)
-    x, k3, lst = walk("a", 3, offs("a", 3), lst, [], float(A))
-    tt(T.QB[:, 0:48], row(x, RVT), T.pta[:, 0:48], GE, k3)
-    w = tt(tm("B3"), row(x, RVT), T.pta[:, 0:48], LT)
-    w = tt(T.QB[:, 48:96], tm("B3"), row(x, RVV), MUL, w)
-    k_pa3 = swap(T.pa3, T.QB, 96, w)
-    tt(tm("N2"), row(X[2], RVT), T.TH[:, 0:48], GE)
-    tt(tm("F1"), tm("E2"), T.pa1[:, 0:48], MUL, k_e2, k_pa1)
-    w = tt(tm("F2"), T.TH[:, 48:96], T.pa1[:, 48:96], ADD)
-    tt(tm("F3"), tm("F1"), tm("F2"), ADD, w)
-    k_z2 = tt(tm("Z2"), tm("N2"), T.pa1[:, 0:48], MUL)
-    x, k4, lst = walk("a", 4, offs("a", 4), lst, [], None)
-    tt(tm("Z3"), tm("Z2"), T.pa3[:, 0:48], MUL, k_z2, k_pa3)
-    w = tt(tm("G1"), tm("Z2"), T.pa3[:, 48:96], MUL)
-    tt(tm("T4"), tm("Z3"), T.TH[:, 0:48], MUL, w)
-    w = tt(tm("G2"), tm("G1"), tm("F3"), ADD)
-    w = tt(tm("B4"), row(x, RVT), tm("T4"), LT, w, k4)
-    w = tt(tm("E4"), tm("B4"), row(x, RVV), MUL, w)
-    for cl in range(2):
-        k_ans = tt(T.ANS[:, cl:48:2], both(tm("E4"), cl), both(tm("G2"), cl), ADD, w)
+    k_t1 = swap(T.p1, T.TH, T.SW, True, True, r_t, k_u)
+    mm(T.p2[:, 0:48], T.EYE[:, :], T.TH[:, 0:48], True, False)
+    swap(T.p3, T.TH, T.SW, True, False)
+    mm(T.p4[:, 0:48], T.EYE[:, :], T.TH[:, 0:48], True, False)
+    mm(T.p6[:, 0:48], T.EYE[:, :], T.TH[:, 48:96], True, False)
 
-    l_f = spread(T.ANS, T.LA[prv], "rF", "lF", k_ans)
-    k_of2 = dma("y", T.LA[prv], T.ANS[:, 6 * me:6 * me + 6], "ownf", k_ans)
+    def arch1(cl, x, k):
+        return nextlist("a", 1, cl, x, k, float(A))
+
+    def arch2(cl, x, k):
+        new = nextlist("a", 2, cl, x, k, float(A))
+        if cl == 0:
+            kh, ke = compare("a", 1, T.p1[:, 0:48], k_t1)
+            S["t2"] = swap(T.p2, T.ha1, T.SWB, False, True, kh)
+            mm(T.p3[:, 0:48], T.EYB[:, :], T.ha1[:, :], False, False)
+            swap(T.p4, T.ha1, T.SWB, False, False)
+            swap(T.p6, T.ea1, T.SW, False, False, ke)
+        else:
+            kh, ke = compare("a", 2, T.p2[:, 0:48], S["t2"])
+            S["t3"] = swap(T.p3, T.ha2, T.SWB, False, True, kh)
+            mm(T.p4[:, 0:48], T.EYB[:, :], T.ha2[:, :], False, False)
+            mm(T.p6[:, 0:48], T.EYE[:, :], T.ea2[:, :], False, False, ke)
+        return new
+
+    def arch3(cl, x, k):
+        new = nextlist("a", 3, cl, x, k, float(A))
+        if cl == 1:
+            kh, ke = compare("a", 3, T.p3[:, 0:48], S["t3"])
+            S["t4"] = swap(T.p4, T.ha3, T.SWB, False, True, kh)
+            S["sum"] = swap(T.p6, T.ea3, T.SW, False, True, ke)
+        return new
+
+    def arch4(cl, x, k):
+        w = tt(both(T.ha4, cl), row(x, ARC + RVT, cl), both(T.p4, cl), LT, k, S["t4"])
+        w = tt(both(T.ea4, cl), both(T.ha4, cl), row(x, ARC + RVV, cl), MUL, w)
+        return tt(T.ANS[:, cl:48:2], both(T.ea4, cl), both(T.p6, cl), ADD, w, S["sum"])
+
+    lst = walk("a", 1, win, [T.AL0[:, :], T.AL1[:, :]], r_n, [k_ar], arch1)
+    lst = walk("a", 2, win, offs("a", 2), lst, [], arch2)
+    lst = walk("a", 3, win, offs("a", 3), lst, [], arch3)
+    k_ans = walk("a", 4, win, offs("a", 4), lst, [], arch4)[1]
+
+    spread(T.ANS, 6, T.RA[:, 6 * prv:6 * prv + 6], "rF", k_ans)
+    k_of2 = dma("y", T.RA[:, 6 * prv:6 * prv + 6], T.ANS[:, 6 * me:6 * me + 6], "ownf", k_ans)
     ends = []
     for cl, nm in ((0, "y"), (1, "s")):
-        for a in range(4):
-            p = 32 * a + 16 * cl
-            k = dma(nm, T.WA[p:p + 1, :], T.LA[:, 32 * a:32 * a + 32, :], "wa%d" % cl, ("rF", into), k_of2, k_w1)
-        ends.append(k)
+        ends.append(dma(nm, T.H[16 * cl:128:32, 0:1536], T.RA[:, :], "wa%d" % cl, ("rF", into), k_of2))
     need("v", ends + [k_ow])
-    yv = done(g.vector.tensor_copy(T.Y0[:, :], T.WA[:, 0:1536].indirect(T.OFW[:, 0:16])), "v", 1)
-    ys = act(T.Y1[:, :], T.WA[:, 0:1536].indirect(T.OFW[:, 16:32]), *(ends + [k_ow]))
+    yv = done(g.vector.tensor_copy(T.Y0[:, :], T.H[:, 0:1536].indirect(T.OFW[:, 0:16])), "v", 1)
+    ys = act(T.Y1[:, :], T.H[:, 0:1536].indirect(T.OFW[:, 16:32]), *(ends + [k_ow]))
     dma("y", T.y[:, 0:256], T.Y0[0:128:16, :], "st0", yv)
     dma("s", T.y[:, 256:512], T.Y1[0:128:16, :], "st1", ys)
-    need("g", [l_b, ("lN", len(es_d)), ("lT", len(es_d)), l_f, r_n, r_t, ("rF", into), ("rB", into)] + list(cnt.items()))
+    need("g", [("lB", sent[0]), r_n[0], r_n[1], r_t, ("rF", into), ("rB", into), r_k] + list(cnt.items()))

@@ -19,11 +19,11 @@ def declare(where, dtype, **shapes):
         SCRATCH[n] = (where, [128, s], dtype)
 
 
-declare("sbuf", "float32", H=HW, AR=AW, RA=48, M32=128, RST=32, OF=4, KF=4, TF=4, O96=4, SC=32, UF=8, LL=512, RK2=96, RT2=96,
-        SNT=24, RBT=24, WW=12, SW=512, EYE=128, X0=384, XT0=384, TE=48, QM=48, MM=48, N4=48, SD=96, TH=96, ANS=48,
-        Y0=256, Y1=256, TLF=1792, CF=24, ZF=512)
-declare("sbuf", "int32", RK=4, RT=4, OI=4, KI=4, SI=4, UI=8, TLI=1792)
-declare("sbuf", "bfloat16", ZB=128, LTI=128, ONE=128, OH=56, EYB=128, SWB=512)
+declare("sbuf", "float32", H=HW, AR=AW, RA=48, M32=128, RST=32, OF=4, KF=4, TF=4, UF=8, LL=512, RR=192,
+        SND=48, RB=48, WW=12, SW=512, EYE=128, X0=384, XT0=384, TE=48, QM=48, MM=48, N4=48, SD=96, TH=96, ANS=48,
+        Y0=256, Y1=256, TLF=1792, CF=24, ZF=256)
+declare("sbuf", "int32", RK=4, RT=4, OI=4, KI=4, SC=32, UI=8, TLI=1792)
+declare("sbuf", "bfloat16", C96=32, ZB=128, LTI=128, ONE=128, OH=56, EYB=128, SWB=512)
 declare("sbuf", "uint16", U0=4, U1=4, OFW=32, SNK=24, L0=24, LST0=24, LST1=24, AL0=24, AL1=24)
 declare("psum", "float32", p0=512, p1=512, p2=512, p3=512, p4=512, p5=512, p6=512, p7=512)
 for _k, _n in (("h", 3), ("a", 4)):
@@ -37,30 +37,31 @@ for _k, _n in (("h", 3), ("a", 4)):
                 SCRATCH["l%s%d%d" % (_k, _i, _c)] = ("sbuf", [128, 24], "uint16")
 SCRATCH["OD"] = ("dram", [2, 128, 4], "uint16")
 SEMAPHORES = ["v", "s", "t", "gp", "ldk", "ldt", "thd", "tvp", "tvt", "tar", "ldh", "ldi", "lda", "ownk", "ownt", "od", "ow",
-              "rK", "rB", "lB", "rN0", "rN1", "rT", "rF", "ownf", "wa0", "wa1", "st0", "st1"]
+              "rK0", "rK1", "rB", "lB", "rN0", "rN1", "rT", "rF", "ownf", "wa0", "wa1", "st0", "st1"]
 
 
-def routes(topo, cores, me):
-    src, n = cores[me], len(cores)
-    near, far = [], []
-    for k in range(1, n):
-        d = (me + k) % n
-        (near if topo.chip(cores[d]) == topo.chip(src) else far).append(d)
-    out, used, call, todo = [], [], 0, list(far)
-    if todo:
-        used = list(topo.engines(src, cores[todo[0]]))
-    while todo:
-        m = 1
-        while m * 2 <= min(len(todo), len(used)):
-            m *= 2
-        per = len(used) // m
-        for i in range(m):
-            out.append((todo[i], used[i * per:(i + 1) * per], call))
-        todo = todo[m:]
-        call += 1
-    for d in near:
-        out.append((d, [e for e in topo.engines(src, cores[d]) if e not in used][:2], 0))
-    return out
+def readers(topo, cores, q):
+    chips = [topo.chip(c) for c in cores]
+    after = [chips[(q + k) % N] for k in range(1, N) if chips[(q + k) % N] != chips[q]][0]
+    one = [r for r in range(N) if chips[r] not in (chips[q], after)]
+    return one + [r for r in range(N) if r not in one]
+
+
+def deal(topo, cores, me, dests):
+    src = cores[me]
+    far = [d for d in dests if topo.chip(cores[d]) != topo.chip(src)]
+    es = topo.engines(src, cores[far[0]])
+    per = len(es) // len(far)
+    out = [(d, es[per * i:per * i + per]) for i, d in enumerate(far)]
+    return out + [(d, [e for e in topo.engines(src, cores[d]) if e not in es][:per]) for d in dests if d not in far]
+
+
+def asks(topo, cores, r, s):
+    return deal(topo, cores, r, [q for q in range(N) if q != r and readers(topo, cores, q).index(r) // 4 == s])
+
+
+def tells(topo, cores, z, s):
+    return deal(topo, cores, z, [r for r in readers(topo, cores, (z - 1) % N)[4 * s:4 * s + 4] if r != z])
 
 
 def bits(es):
@@ -112,9 +113,9 @@ def rank_program(g, core, T, topo):
         need("v", toks)
         return done(g.vector.transpose(out, a), "v", 1)
 
-    def act(out, a, *toks):
+    def act(out, a, *toks, bias=0.0):
         need("s", toks)
-        return done(g.scalar.activation(out, a, COPY), "s", 1)
+        return done(g.scalar.activation(out, a, COPY, bias=bias), "s", 1)
 
     def mm(out, l, r, start, stop, *toks):
         need("t", toks)
@@ -124,13 +125,13 @@ def rank_program(g, core, T, topo):
         need(name, toks)
         return done(q[name].dma_start(out, src), sem, 16)
 
-    def swap(out, src, mat, start, stop, *toks):
+    def swap(out, src, mat, start, stop, *toks, lo=0, hi=48):
         tk = None
         for gs in range(2):
             for G in range(2):
                 k = 256 * gs + 128 * G
-                tk = mm(out[:, gs:48:2], mat[:, k:k + 128], src[:, G:48:2], start and gs + G == 0, stop and gs + G == 2,
-                        *toks)
+                tk = mm(out[:, lo + gs:hi:2], mat[:, k:k + 128], src[:, lo + G:hi:2], start and gs + G == 0,
+                        stop and gs + G == 2, *toks)
         return tk
 
     def iota(out, pat, base, cm, **kw):
@@ -143,25 +144,31 @@ def rank_program(g, core, T, topo):
     fl = {"allow_small_or_imprecise_dtypes": True}
     k_rk = dma("y", T.RK[:, :], T.rk[:, :], "ldk")
     k_rt = dma("s", T.RT[:, :], T.rt[:, :], "ldt")
-    tiles = {"hd": (0, 1), "vp": (256, 2), "vt": (768, 2), "ap": (1280, 1), "at": (1536, 1)}
+    CH = 2048
+    tiles = {"hd": (0, K), "vp": (256, V), "vt": (768, V), "ap": (1280, A), "at": (1536, A)}
+    pieces = [(0, K), (K, K + CH), (K + CH, V)]
 
-    def tile(buf, name, piece, cl):
+    def tile(buf, name, lo, hi, cl):
         c0, n = tiles[name]
-        p0, h = 64 // n * (2 * piece + cl), 64 // n
-        return buf[p0:p0 + h, c0:c0 + 256 * n]
+        p0, h = 128 * lo // n, 64 * (hi - lo) // n
+        return buf[p0 + h * cl:p0 + h * cl + h, c0:c0 + n // 16]
 
-    k_tl = {}
-    for name, sem in (("hd", "thd"), ("vp", "tvp"), ("vt", "tvt"), ("ap", "tar"), ("at", "tar")):
-        for piece in range(tiles[name][1]):
-            for cl in range(2):
-                k_tl[name] = dma("y", tile(T.TLI, name, piece, cl), T[name][cl:8:2, A * piece:A * piece + A], sem)
+    def fetch(queue, name, sem):
+        for lo, hi in pieces:
+            for cl in range(2 if hi <= tiles[name][1] else 0):
+                k = dma(queue, tile(T.TLI, name, lo, hi, cl), T[name][cl:8:2, lo:hi], sem)
+        return k
+
+    k_tl = {name: fetch("y", name, "t" + name) for name in ("hd", "vp", "vt")}
     z0 = fill(T.ZB[:, :], 0.0)
     f0 = fill(T.ZF[:, :], 0.0)
     i_m = iota(T.M32[:, :], [[0, 4], [1, 32]], 0, 0, **fl)
     pick(T.LTI[:, :], T.ZB[:, :], [[-1, 128]], GE, 1.0, 0, 1, z0)
-    k_lti = pick(T.EYB[:, :], T.ZB[:, :], [[1, 128]], NE, -BIG, 0, -1)
-    G0, V0, V1 = 3072, 768, 6144
+    pick(T.EYB[:, :], T.ZB[:, :], [[1, 128]], NE, -BIG, 0, -1)
+    i_c = iota(T.C96[:, :], [[0, 4], [96, 8]], 0, 0, **fl)
+    G0, G1, V0, S2, V1 = 3456, 5632, 768, 4864, 7168
     i_h = iota(T.H[:, G0:K], [[0, K - G0]], 0, 0, **fl)
+    i_g = iota(T.H[:, G1:3 * CH], [[0, 3 * CH - G1]], 0, 0, **fl)
 
     z1 = fill(T.ONE[:, :], 1.0)
     z2 = fill(T.OH[:, 0:24], 0.0)
@@ -170,76 +177,72 @@ def rank_program(g, core, T, topo):
     fill(T.RST[:, 0:32:8], 0.0, w)
 
     def sfill(lo, hi, *toks):
-        for a0 in range(lo, hi, 512):
-            n = min(512, hi - a0)
+        for a0 in range(lo, hi, 256):
+            n = min(256, hi - a0)
             k = act(T.H[:, a0:a0 + n], T.ZF[:, 0:n], *toks)
         return k
 
     def convert(name):
         c0, n = tiles[name]
-        return act(T.TLF[:, c0:c0 + 256 * n], T.TLI[:, c0:c0 + 256 * n], k_tl[name])
+        return act(T.TLF[:, c0:c0 + n // 16], T.TLI[:, c0:c0 + n // 16], k_tl[name], bias=0.0 if name == "vt" else -float(V))
 
-    s_1 = sfill(V0, 2048, f0)
-    c_hd = convert("hd")
-    sfill(2048, 2560)
-    c_vp = convert("vp")
-    s_2 = sfill(2560, G0)
-    c_vt = convert("vt")
-    s_3 = sfill(K, V1)
+    s_f = [sfill(V0, CH, f0), sfill(CH, G0)]
+    s_c = {name: convert(name) for name in ("hd", "vp", "vt")}
+    s_f += [sfill(K, S2), sfill(3 * CH, V1)]
 
     w = ts(T.OI[:, :], T.RK[:, :], 12, None, SHR, None, k_rk)
     k_of = cp(T.OF[:, :], T.OI[:, :], w)
     for f in range(4):
         k_oh = ts(T.OH[:, 24 + 8 * f:32 + 8 * f], T.M32[:, 0:8], T.OF[:, f:f + 1], None, EQ, None, k_of, z2, i_m)
-    mm(T.p0[:, 0:32], T.LTI[:, :], T.OH[:, 24:56], True, False, k_lti, k_oh)
+    mm(T.p0[:, 0:32], T.ONE[0:1, :], T.C96[0:1, :], True, False, z1, i_c)
+    mm(T.p0[:, 0:32], T.LTI[:, :], T.OH[:, 24:56], False, False, k_oh)
     mm(T.p0[:, 0:32], T.EYB[:, :], T.OH[:, 24:56], False, False)
     for d in (1, 2, 3):
-        m = mm(T.p0[:, 0:32], T.ONE[:, :], T.OH[:, 24 - 8 * d:56 - 8 * d], False, d == 3, z1)
+        m = mm(T.p0[:, 0:32], T.ONE[:, :], T.OH[:, 24 - 8 * d:56 - 8 * d], False, d == 3)
     w = ts(T.KI[:, :], T.RK[:, :], 4095, None, AND, None)
-    k_o96 = ts(T.O96[:, :], T.OF[:, :], 96.0, BIG, MUL, ADD)
+    k_tf = ts(T.TF[:, :], T.RT[:, :], 1.0, None, ADD, None, k_rt)
     k_kf = cp(T.KF[:, :], T.KI[:, :], w)
-    need("v", [m, k_o96])
+    need("v", [m])
     w = done(g.vector.tensor_tensor_scan(T.SC[:, :], T.RST[:, :], T.p0[:, 0:32], 0.0, MUL, MIN), "v", 1)
-    w = tt(T.SI[:, :], T.SC[:, 7:32:8], T.O96[:, :], ADD, w)
-    ts(T.UI[:, 0:4], T.SI[:, :], 31, None, AND, None, w)
-    w = ts(T.UI[:, 4:8], T.SI[:, :], 5, None, SHR, None)
+    ts(T.UI[:, 0:4], T.SC[:, 7:32:8], 31, None, AND, None, w)
+    w = ts(T.UI[:, 4:8], T.SC[:, 7:32:8], 5, 31, SHR, AND)
     k_uf = cp(T.UF[:, :], T.UI[:, :], w)
     for f in range(4):
-        ts(T.RK2[:, 24 * f:24 * f + 24], T.M32[:, 0:24], T.UF[:, 4 + f:5 + f], T.KF[:, f:f + 1], EQ, MUL, k_uf)
+        for j, val in enumerate((T.KF, T.TF)):
+            ts(T.RR[:, 48 * f + j:48 * f + 48:2], T.M32[:, 0:24], T.UF[:, 4 + f:5 + f], val[:, f:f + 1], EQ, MUL, k_uf)
         w = ts(T.LL[:, 128 * f:128 * f + 128], T.M32[:, :], T.UF[:, f:f + 1], None, EQ, None)
-        m = mm(T.p1[:, 0:24], T.LL[:, 128 * f:128 * f + 128], T.RK2[:, 24 * f:24 * f + 24], f == 0, f == 3, w)
-    k_tf = ts(T.TF[:, :], T.RT[:, :], 1.0, None, ADD, None, k_rt)
-    k_snk = cp(T.SNK[:, :], T.p1[:, 0:24], m)
-    for f in range(4):
-        w = ts(T.RT2[:, 24 * f:24 * f + 24], T.M32[:, 0:24], T.UF[:, 4 + f:5 + f], T.TF[:, f:f + 1], EQ, MUL, k_tf)
-        m = mm(T.p2[:, 0:24], T.LL[:, 128 * f:128 * f + 128], T.RT2[:, 24 * f:24 * f + 24], f == 0, f == 3, w)
-    fill(T.H[:, V1:V1 + 512], 0.0)
-    k_snt = cp(T.SNT[:, :], T.p2[:, 0:24], m)
-    fill(T.CF[:, 0:8], float(V))
+        m = mm(T.p1[:, 0:48], T.LL[:, 128 * f:128 * f + 128], T.RR[:, 48 * f:48 * f + 48], f == 0, f == 3, w)
+    fill(T.H[:, S2:S2 + 256], 0.0)
+    k_snd = cp(T.SND[:, :], T.p1[:, 0:48], m)
+    f3 = fill(T.H[:, S2 + 256:G1], 0.0)
+    f2 = fill(T.H[:, V1:HW], 0.0)
     fill(T.CF[:, 8:16], float(A))
     fill(T.CF[:, 16:24], BIG)
-    fill(T.AR[:, A:AW], 0.0)
-    f2 = fill(T.H[:, V1 + 512:HW], 0.0)
-    c_ar = cp(T.TLF[:, 1280:1792], T.TLI[:, 1280:1792], k_tl["at"])
+    k_cf = fill(T.AR[:, A:AW], 0.0)
 
-    mine = routes(topo, cores, me)
     sent = [0]
 
-    def spread(src, n, dst, rsem, tok):
+    def spread(plan, src, dst, rsem, tok):
         need("g", [tok])
-        for call in range(1 + max(c for _, _, c in mine)):
-            trs = []
-            for d, es, c in mine:
-                if c == call:
-                    rid, pid, _ = topo.addr(cores[d])
-                    trs.append(RemoteDMATransfer(dst_ids=[DstId(rid=rid, pnc=pid)], dma_engine_mask=bits(es), alu_op=0,
-                                                 remote_sem=T.sem[rsem], srcs=[src[:, n * d:n * d + n]], dsts=[dst]))
-                    sent[0] += len(es)
-            g.remote_dma_fused(trs, local_sem=T.sem.lB)
+        trs = []
+        for d, es in plan:
+            rid, pid, _ = topo.addr(cores[d])
+            trs.append(RemoteDMATransfer(dst_ids=[DstId(rid=rid, pnc=pid)], dma_engine_mask=bits(es), alu_op=0,
+                                         remote_sem=T.sem[rsem], srcs=[src(d)], dsts=[dst(d)]))
+            sent[0] += len(es)
+        g.remote_dma_fused(trs, local_sem=T.sem.lB)
 
-    into = sum(len(es) for r in range(N) if r != me for d, es, _ in routes(topo, cores, r) if d == me)
-    spread(T.SNK, 3, T.L0[:, 3 * me:3 * me + 3], "rK", k_snk)
-    spread(T.SNT, 3, T.RBT[:, 3 * me:3 * me + 3], "rB", k_snt)
+    def arrivals(calls, streams):
+        return sum(len(es) for r in range(N) for s in streams for d, es in calls(topo, cores, r, s) if d == me)
+
+    def slot(buf, q, r):
+        k = readers(topo, cores, q).index(r)
+        return buf[:, 6 * k:6 * k + 6]
+
+    for s in range(2):
+        spread(asks(topo, cores, me, s), lambda d: T.SND[:, 6 * d:6 * d + 6], lambda d: slot(T.RB, d, me), "rK%d" % s, k_snd)
+    r_k = [("rK%d" % s, arrivals(asks, [s])) for s in range(2)]
+    r_f = ("rF", arrivals(tells, [0, 1]))
 
     k_eye = pick(T.EYE[:, :], T.ZF[:, 0:128], [[1, 128]], NE, 1.0, 0, -1, f0)
     for mat, zero, val in ((T.SW, T.ZF, 1.0), (T.SWB, T.ZB, -BIG)):
@@ -262,30 +265,30 @@ def rank_program(g, core, T, topo):
     def cols(t, lo, hi):
         return lambda cl: t[cl:8:2, lo:hi]
 
-    def conv(name, piece):
-        return lambda cl: tile(T.TLF, name, piece, cl)
+    def table(name, lo, hi, sem, *toks):
+        return rows(lo, hi, lambda cl: tile(T.TLF, name, lo, hi, cl), place[name], sem, *toks)
 
-    rows(0, 2048, cols(T.vv, 0, 2048), RVV, "ldh", f1, s_1)
-    rows(2048, K, cols(T.vv, 2048, K), RVV, "ldh", s_2, i_h)
-    rows(0, K, conv("hd", 0), RHD, "ldh", c_hd)
-    rows(0, K, conv("vp", 0), RVP, "ldh", c_vp)
-    k_h0 = rows(0, K, conv("vt", 0), RVT, "ldh", c_vt)
-    k_own = dma("y", T.L0[:, 3 * me:3 * me + 3], T.SNK[:, 3 * me:3 * me + 3], "ownk", k_snk)
-    rows(K, V1, cols(T.vv, K, V1), RVV, "ldi", s_3)
-    rows(K, V, conv("vp", 1), RVP, "ldi", f2)
-    rows(K, V, conv("vt", 1), RVT, "ldi")
-    rows(V1, V, cols(T.vv, V1, V), RVV, "ldi")
-    dma("y", T.H[RVP:128:8, V:HW], T.CF[0:16, 0:8], "ldi")
-    k_h = dma("y", T.H[RVT:128:8, V:HW], T.CF[0:16, 16:24], "ldi")
-    k_ownt = dma("y", T.RBT[:, 3 * me:3 * me + 3], T.SNT[:, 3 * me:3 * me + 3], "ownt", k_snt)
+    place = {"hd": RHD, "vp": RVP, "vt": RVT, "ap": RVP, "at": RVT}
+    for i, toks in enumerate(([f1], [i_h], [i_g, f3], [f2])):
+        sem = "ldh" if i < 2 else "ldi"
+        rows(CH * i, CH * i + CH, cols(T.vv, CH * i, CH * i + CH), RVV, sem, s_f[i], *toks)
+        for name in ([], ["hd", "vp", "vt"], ["vp", "vt"], ["vp", "vt"])[i]:
+            k = table(name, *pieces[i - 1], sem, s_c[name])
+        if i == 1:
+            k_h0 = k
+            k_own = dma("y", slot(T.RB, me, me), T.SND[:, 6 * me:6 * me + 6], "ownk", k_snd)
+        if i == 0:
+            fetch("y", "ap", "tar")
+            c_ar = act(T.TLF[:, 1280:1792], T.TLI[:, 1280:1792], fetch("y", "at", "tar"))
+    k_h = dma("y", T.H[RVT:128:8, V:HW], T.CF[0:16, 16:24], "ldi", k_cf)
     win = T.AR
     rows(0, A, cols(T.av, 0, A), RVV, "lda")
-    rows(0, A, conv("ap", 0), RVP, "lda", c_ar)
-    rows(0, A, conv("at", 0), RVT, "lda")
     for r in range(RVV + 1, 8):
         dma("y", T.AR[r:128:8, 0:A], T.vv[:, :], "lda")
     dma("y", T.AR[RVP:128:8, A:AW], T.CF[0:16, 8:16], "lda")
-    k_ar = dma("y", T.AR[RVT:128:8, A:AW], T.CF[0:16, 16:24], "lda")
+    dma("y", T.AR[RVT:128:8, A:AW], T.CF[0:16, 16:24], "lda")
+    table("ap", 0, A, "lda", c_ar)
+    k_ar = table("at", 0, A, "lda")
 
     def row(x, r, cl=None):
         a = 8 + r + (384 * cl if cl else 0)
@@ -294,16 +297,32 @@ def rank_program(g, core, T, topo):
     def both(x, cl):
         return x[:, 24 * cl:24 * cl + 24]
 
-    def hd_row(cl):
-        return T.XT0[:, RHD + 8 * cl:RHD + 8 * cl + 369:16]
+    def part(x, s, c):
+        return x[:, 24 * s + 12 * c:24 * s + 12 * c + 12]
 
-    r_k = ("rK", into)
-    need("v", [r_k, k_own, k_h0])
-    g0 = done(g.vector.tensor_copy(T.X0[:, 0:192], T.H[:, 0:K].indirect(T.L0[:, 0:12])), "v", 1)
-    g1 = act(T.X0[:, 192:384], T.H[:, 0:K].indirect(T.L0[:, 12:24]), r_k, k_own, k_h0)
-    w = tr(T.XT0[:, :], T.X0[:, :], g0, g1)
-    lst = [ts(T["lh1%d" % cl][:, :], hd_row(cl), float(V), None, MIN, None, w) for cl in range(2)]
-    X, first = {}, {"h": 0, "a": ARC}
+    def hd_row(s, c):
+        a = 192 * s + RHD + 8 * (1 - c)
+        return T.XT0[:, a:a + 177:16]
+
+    lst, got = [], []
+    for s in range(2):
+        lo = 12 * s
+        w = cp(T.L0[:, lo:lo + 12], T.RB[:, 2 * lo:2 * lo + 24:2], r_k[s], *([k_own] if s else []))
+        if s == 0:
+            got = [act(T.X0[:, 96:192], T.H[:, 0:K].indirect(T.L0[:, 6:12]), w, k_h0)]
+            got.append(cp(T.X0[:, 0:96], T.H[:, 0:K].indirect(T.L0[:, 0:6]), w, k_h0))
+        else:
+            cp(part(T.TE, 0, 0), T.RB[:, 1:24:2])
+            got = [cp(T.X0[:, 192:384], T.H[:, 0:K].indirect(T.L0[:, 12:24]), w)]
+            cp(part(T.TE, 0, 1), T.RB[:, 1:24:2])
+        w = tr(T.XT0[:, 192 * s:192 * s + 192], T.X0[:, 192 * s:192 * s + 192], *got)
+        if s == 1:
+            cp(part(T.TE, 1, 0), T.RB[:, 25:48:2])
+        for c in range(2):
+            k = ts(T["lh1%d" % s][:, 12 * c:12 * c + 12], hd_row(s, c), float(V), float(V), ADD, MIN, w)
+        lst.append(k)
+
+    X, first = {}, {"h": float(V), "a": 0.0}
 
     def walk(kind, i, win, offs, toks, extra, after):
         x = X[i] = T["X%s%d" % (kind, i)]
@@ -311,8 +330,9 @@ def rank_program(g, core, T, topo):
         for cl in range(2):
             buf = T["g%s%d%d" % (kind, i, cl)]
             a = act(buf[:, :], win.indirect(offs[cl]), toks[cl], *extra)
-            o = 384 if cl else 8
-            k = tr(x[:, o:o + 384], buf[:, :], *([a] + ([k] if k else [])))
+            o = 384 * cl
+            tr(x[:, o:o + 192], buf[:, 0:192], *([a] + ([k] if k else [])))
+            k = tr(x[:, o + 200:o + 392], buf[:, 192:384])
             new.append(after(cl, x, k))
         return new
 
@@ -320,41 +340,41 @@ def rank_program(g, core, T, topo):
         return [T["l%s%d%d" % (kind, i, cl)][:, 0:24] for cl in range(2)]
 
     def nextlist(kind, i, cl, x, k, cap):
-        return ts(T["l%s%d%d" % (kind, i + 1, cl)][:, :], row(x, first[kind] + RVP, cl), cap, None, MIN, None, k)
+        return ts(T["l%s%d%d" % (kind, i + 1, cl)][:, :], row(x, RVP, cl), first[kind], cap, ADD, MIN, k)
 
-    def compare(kind, i, open_t, *toks):
-        h, e = T["h%s%d" % (kind, i)], T["e%s%d" % (kind, i)]
-        kh = tt(h[:, :], row(X[i], first[kind] + RVT), open_t, LT, *toks)
-        return kh, tt(e[:, :], h[:, :], row(X[i], first[kind] + RVV), MUL, kh)
+    def stops(kind, i, open_t, *toks):
+        return tt(T["h%s%d" % (kind, i)][:, :], row(X[i], RVT), open_t, LT, *toks)
+
+    def gives(kind, i, *toks):
+        return tt(T["e%s%d" % (kind, i)][:, :], T["h%s%d" % (kind, i)][:, :], row(X[i], RVV), MUL, *toks)
 
     S = {}
     win = T.H[:, 0:HW]
+    pm = (T.p5, T.p7)
 
     def heap1(cl, x, k):
-        new = nextlist("h", 1, cl, x, k, float(V))
         if cl == 0:
-            cp(T.TE[:, 0:24], T.RBT[:, :], ("rB", into), k_ownt)
-            S["te"] = cp(T.TE[:, 24:48], T.RBT[:, :])
-            swap(T.p1, T.TE, T.SW, True, False, S["te"], k_sw)
+            swap(T.p1, T.TE, T.SW, True, False, cp(part(T.TE, 1, 1), T.RB[:, 25:48:2]), k_sw)
             mm(T.p2[:, 0:48], T.EYE[:, :], T.TE[:, :], True, False, k_eye)
             mm(T.p3[:, 0:48], T.EYE[:, :], T.TE[:, :], True, False)
-        else:
-            kh, ke = compare("h", 1, T.TE[:, :], S["te"], k)
-            S["t2"] = swap(T.p1, T.hh1, T.SWB, False, True, kh, k_swb)
+        new = nextlist("h", 1, cl, x, k, float(V))
+        if cl == 1:
+            S["h"] = stops("h", 1, T.TE[:, :])
+            S["t2"] = swap(T.p1, T.hh1, T.SWB, False, True, S["h"], k_swb)
             mm(T.p2[:, 0:48], T.EYB[:, :], T.hh1[:, :], False, False)
             mm(T.p3[:, 0:48], T.EYB[:, :], T.hh1[:, :], False, False)
-            mm(T.p4[:, 0:48], T.EYE[:, :], T.eh1[:, :], True, False, ke)
         return new
 
     def heap2(cl, x, k):
+        if cl == 0:
+            gives("h", 1, S["h"])
         new = nextlist("h", 2, cl, x, k, float(V))
-        w = tt(both(T.QM, cl), hd_row(cl), row(x, RVP, cl), MAX)
+        for c in range(2):
+            a = 8 + RVP + 384 * cl + 192 * c
+            w = tt(part(T.QM, cl, c), hd_row(cl, c), x[:, a:a + 177:16], MAX)
         if cl == 1:
-            S["pm"] = swap(T.p5, T.QM, T.SW, True, True, w)
-            kh, ke = compare("h", 2, T.p1[:, 0:48], S["t2"])
-            S["t3"] = swap(T.p2, T.hh2, T.SWB, False, True, kh)
-            swap(T.p3, T.hh2, T.SWB, False, False)
-            S["v2"] = swap(T.p4, T.eh2, T.SW, False, True, ke)
+            S["mm0"] = tt(both(T.MM, 0), row(X[1], RVP, 0), both(pm[0], 0), MAX, S["pm0"])
+        S["pm%d" % cl] = swap(pm[cl], T.QM, T.SW, True, True, w, lo=24 * cl, hi=24 * cl + 24)
         return new
 
     zc = cores[nxt]
@@ -370,18 +390,26 @@ def rank_program(g, core, T, topo):
 
     def heap3(cl, x, k):
         if cl == 0:
-            S["mm"] = tt(T.MM[:, :], row(X[1], RVP), T.p5[:, 0:48], MAX, S["pm"])
-        w = tt(both(T.N4, cl), row(x, RVP, cl), both(T.MM, cl), MAX, k, S["mm"])
-        w = ts(T["LST%d" % cl][:, :], both(T.N4, cl), -float(V), None, ADD, None, w)
+            S["h"] = stops("h", 2, T.p1[:, 0:48], S["t2"])
+            S["t3"] = swap(T.p2, T.hh2, T.SWB, False, True, S["h"])
+            swap(T.p3, T.hh2, T.SWB, False, False)
+            mm(T.p4[:, 0:48], T.EYE[:, :], T.eh1[:, :], True, False)
+        else:
+            S["v2"] = swap(T.p4, T.eh2, T.SW, False, True, gives("h", 2, S["h"]))
+        w = tt(T["LST%d" % cl][:, :], row(x, RVP, cl), both(T.MM, cl), MAX, k, S["mm%d" % cl])
+        if cl == 0:
+            S["mm1"] = tt(both(T.MM, 1), row(X[1], RVP, 1), both(pm[1], 1), MAX, S["pm1"])
+        else:
+            S["h"] = stops("h", 3, T.p2[:, 0:48], S["t3"])
         return onward(T["AL%d" % cl][:, :], T["LST%d" % cl][:, :], "rN%d" % cl, w)
 
     lst = walk("h", 1, win, offs("h", 1), lst, [k_h], heap1)
     lst = walk("h", 2, win, offs("h", 2), lst, [], heap2)
     r_n = walk("h", 3, win, offs("h", 3), lst, [], heap3)
-    kh, ke = compare("h", 3, T.p2[:, 0:48], S["t3"])
-    k_t4 = mm(T.p3[:, 0:48], T.EYB[:, :], T.hh3[:, :], False, True, kh)
-    tt(T.SD[:, 48:96], T.eh3[:, :], T.p4[:, 0:48], ADD, ke, S["v2"])
-    w = cp(T.SD[:, 0:48], T.p3[:, 0:48], k_t4)
+    k_t4 = mm(T.p3[:, 0:48], T.EYB[:, :], T.hh3[:, :], False, True, S["h"])
+    ke = gives("h", 3, S["h"])
+    cp(T.SD[:, 0:48], T.p3[:, 0:48], k_t4)
+    w = tt(T.SD[:, 48:96], T.eh3[:, :], T.p4[:, 0:48], ADD, ke, S["v2"])
     r_t = onward(T.TH[:, :], T.SD[:, :], "rT", w)
     ts(T.WW[:, 0:4], T.UF[:, 0:4], 48.0, None, MUL, None)
     w = ts(T.WW[:, 4:8], T.UF[:, 4:8], 2.0, None, MUL, None)
@@ -396,54 +424,75 @@ def rank_program(g, core, T, topo):
     win = T.AR[:, 0:AW]
     k_t1 = swap(T.p1, T.TH, T.SW, True, True, r_t, k_u)
     mm(T.p2[:, 0:48], T.EYE[:, :], T.TH[:, 0:48], True, False)
-    swap(T.p3, T.TH, T.SW, True, False)
-    mm(T.p4[:, 0:48], T.EYE[:, :], T.TH[:, 0:48], True, False)
-    mm(T.p6[:, 0:48], T.EYE[:, :], T.TH[:, 48:96], True, False)
 
     def arch1(cl, x, k):
         return nextlist("a", 1, cl, x, k, float(A))
 
     def arch2(cl, x, k):
+        if cl == 0:
+            S["h"] = stops("a", 1, T.p1[:, 0:48], k_t1)
+            S["t2"] = swap(T.p2, T.ha1, T.SWB, False, True, S["h"])
+            mm(T.p3[:, 0:48], T.EYB[:, :], T.ha1[:, :], True, False)
+            swap(T.p3, T.TH, T.SW, False, False)
         new = nextlist("a", 2, cl, x, k, float(A))
         if cl == 0:
-            kh, ke = compare("a", 1, T.p1[:, 0:48], k_t1)
-            S["t2"] = swap(T.p2, T.ha1, T.SWB, False, True, kh)
-            mm(T.p3[:, 0:48], T.EYB[:, :], T.ha1[:, :], False, False)
-            swap(T.p4, T.ha1, T.SWB, False, False)
-            swap(T.p6, T.ea1, T.SW, False, False, ke)
+            gives("a", 1, S["h"])
         else:
-            kh, ke = compare("a", 2, T.p2[:, 0:48], S["t2"])
-            S["t3"] = swap(T.p3, T.ha2, T.SWB, False, True, kh)
-            mm(T.p4[:, 0:48], T.EYB[:, :], T.ha2[:, :], False, False)
-            mm(T.p6[:, 0:48], T.EYE[:, :], T.ea2[:, :], False, False, ke)
+            S["h"] = stops("a", 2, T.p2[:, 0:48], S["t2"])
+            S["t3"] = swap(T.p3, T.ha2, T.SWB, False, True, S["h"])
+            mm(T.p4[:, 0:48], T.EYB[:, :], T.ha2[:, :], True, False)
+            swap(T.p4, T.ha1, T.SWB, False, False)
+            mm(T.p4[:, 0:48], T.EYE[:, :], T.TH[:, 0:48], False, False)
+            mm(T.p6[:, 0:48], T.EYE[:, :], T.TH[:, 48:96], True, False)
+            swap(T.p6, T.ea1, T.SW, False, False)
         return new
 
     def arch3(cl, x, k):
+        if cl == 0:
+            mm(T.p6[:, 0:48], T.EYE[:, :], T.ea2[:, :], False, False, gives("a", 2, S["h"]))
         new = nextlist("a", 3, cl, x, k, float(A))
         if cl == 1:
-            kh, ke = compare("a", 3, T.p3[:, 0:48], S["t3"])
-            S["t4"] = swap(T.p4, T.ha3, T.SWB, False, True, kh)
-            S["sum"] = swap(T.p6, T.ea3, T.SW, False, True, ke)
+            S["h"] = stops("a", 3, T.p3[:, 0:48], S["t3"])
+            S["t4"] = swap(T.p4, T.ha3, T.SWB, False, True, S["h"])
+            S["sum"] = swap(T.p6, T.ea3, T.SW, False, True, gives("a", 3, S["h"]))
         return new
-
-    def arch4(cl, x, k):
-        w = tt(both(T.ha4, cl), row(x, ARC + RVT, cl), both(T.p4, cl), LT, k, S["t4"])
-        w = tt(both(T.ea4, cl), both(T.ha4, cl), row(x, ARC + RVV, cl), MUL, w)
-        return tt(T.ANS[:, cl:48:2], both(T.ea4, cl), both(T.p6, cl), ADD, w, S["sum"])
 
     lst = walk("a", 1, win, [T.AL0[:, :], T.AL1[:, :]], r_n, [k_ar], arch1)
     lst = walk("a", 2, win, offs("a", 2), lst, [], arch2)
     lst = walk("a", 3, win, offs("a", 3), lst, [], arch3)
-    k_ans = walk("a", 4, win, offs("a", 4), lst, [], arch4)[1]
 
-    spread(T.ANS, 6, T.RA[:, 6 * prv:6 * prv + 6], "rF", k_ans)
-    k_of2 = dma("y", T.RA[:, 6 * prv:6 * prv + 6], T.ANS[:, 6 * me:6 * me + 6], "ownf", k_ans)
+    x = T.Xa4
+
+    def hit(s, *toks):
+        return tt(both(T.ha4, s), row(x, RVT, s), both(T.p4, s), LT, S["t4"], *toks)
+
+    def value(s, *toks):
+        return tt(both(T.ea4, s), both(T.ha4, s), row(x, RVV, s), MUL, *toks)
+
+    def tell(s, *toks):
+        for c in range(2):
+            k = tt(T.ANS[:, 24 * s + 1 - c:24 * s + 24:2], part(T.ea4, s, c), part(T.p6, s, c), ADD, S["sum"], *toks)
+        spread(tells(topo, cores, me, s), lambda d: slot(T.ANS, prv, d), lambda d: T.RA[:, 6 * prv:6 * prv + 6], "rF", k)
+        return k
+
+    a0 = act(T.ga40[:, :], win.indirect(T.la40[:, :]), lst[0])
+    a1 = act(T.ga41[:, 0:192], win.indirect(T.la41[:, 0:12]), lst[1])
+    a2 = act(T.ga41[:, 192:384], win.indirect(T.la41[:, 12:24]))
+    tr(x[:, 0:192], T.ga40[:, 0:192], a0)
+    w = hit(0, tr(x[:, 200:392], T.ga40[:, 192:384]))
+    tr(x[:, 384:576], T.ga41[:, 0:192], a1)
+    w = value(0, w)
+    k = tr(x[:, 584:776], T.ga41[:, 192:384], a2)
+    tell(0, w)
+    k_ans = tell(1, value(1, hit(1, k)))
+
+    k_of2 = dma("y", T.RA[:, 6 * prv:6 * prv + 6], slot(T.ANS, prv, me), "ownf", k_ans)
     ends = []
     for cl, nm in ((0, "y"), (1, "s")):
-        ends.append(dma(nm, T.H[16 * cl:128:32, 0:1536], T.RA[:, :], "wa%d" % cl, ("rF", into), k_of2))
+        ends.append(dma(nm, T.H[16 * cl:128:32, 0:1536], T.RA[:, :], "wa%d" % cl, r_f, k_of2))
     need("v", ends + [k_ow])
     yv = done(g.vector.tensor_copy(T.Y0[:, :], T.H[:, 0:1536].indirect(T.OFW[:, 0:16])), "v", 1)
     ys = act(T.Y1[:, :], T.H[:, 0:1536].indirect(T.OFW[:, 16:32]), *(ends + [k_ow]))
     dma("y", T.y[:, 0:256], T.Y0[0:128:16, :], "st0", yv)
     dma("s", T.y[:, 256:512], T.Y1[0:128:16, :], "st1", ys)
-    need("g", [("lB", sent[0]), r_n[0], r_n[1], r_t, ("rF", into), ("rB", into), r_k] + list(cnt.items()))
+    need("g", [("lB", sent[0]), r_n[0], r_n[1], r_t, r_f] + r_k + list(cnt.items()))

@@ -4,12 +4,21 @@ from concourse.mybir import dt, AluOpType, AxisListType, ActivationFunctionType
 N, K, V, A, R = 8, 4096, 8192, 4096, 512
 HW = V + 8
 BIG = 2097152.0
+M4096, M64 = 1.5 * 2.0 ** 35, 1.5 * 2.0 ** 29
 RVP, RVT, RVV, RHD = 0, 1, 2, 3
-ARC, AW = 0, A + 8
+AW = A + 8
+SRC = 512
+FILL = [("c", 2304), ("v", 256), ("s", 1280), ("s", 256), ("g", 384), ("s", 1152), ("w", 512), ("s", 768), ("w", 768)]
+CONVERT = [["hd"], ["vp", "vt"], [], []]
+PIECES = [(0, K), (K, 6144), (6144, V)]
+LOADS = [("copies", 0, FILL[0][1]), ("end", V, HW), ("vv", 0, K), ("hd", 0, K)]
+LOADS += [(name, lo, hi) for lo, hi in PIECES for name in ("vp", "vt")]
+LOADS.insert(-2, ("vv", K, V))
+NS, W = 3, 8
 COPY = ActivationFunctionType.Copy
 ADD, SUB, MUL, MAX, MIN = AluOpType.add, AluOpType.subtract, AluOpType.mult, AluOpType.max, AluOpType.min
-GE, GT, LT, EQ, NE = AluOpType.is_ge, AluOpType.is_gt, AluOpType.is_lt, AluOpType.is_equal, AluOpType.not_equal
-SHR, AND = AluOpType.arith_shift_right, AluOpType.bitwise_and
+GE, LT, EQ, NE = AluOpType.is_ge, AluOpType.is_lt, AluOpType.is_equal, AluOpType.not_equal
+AND = AluOpType.bitwise_and
 
 SCRATCH = {}
 
@@ -19,32 +28,36 @@ def declare(where, dtype, **shapes):
         SCRATCH[n] = (where, [128, s], dtype)
 
 
-declare("sbuf", "float32", H=HW, AR=AW, RA=48, M32=128, RST=32, OF=4, KF=4, TF=4, UF=8, LL=512, RR=192,
-        SND=48, RB=48, WW=12, SW=512, EYE=128, X0=384, XT0=384, TE=48, QM=48, MM=48, N4=48, SD=96, TH=96, ANS=48,
-        Y0=256, Y1=256, TLF=1792, CF=24, ZF=256)
-declare("sbuf", "int32", RK=4, RT=4, OI=4, KI=4, SC=32, UI=8, TLI=1792)
-declare("sbuf", "bfloat16", C96=32, ZB=128, LTI=128, ONE=128, OH=56, EYB=128, SWB=512)
-declare("sbuf", "uint16", U0=4, U1=4, OFW=32, SNK=24, L0=24, LST0=24, LST1=24, AL0=24, AL1=24)
-declare("psum", "float32", p0=512, p1=512, p2=512, p3=512, p4=512, p5=512, p6=512, p7=512)
-for _k, _n in (("h", 3), ("a", 4)):
-    for _i in range(1, _n + 1):
-        SCRATCH["X%s%d" % (_k, _i)] = ("sbuf", [128, 776], "float32")
-        SCRATCH["h%s%d" % (_k, _i)] = ("sbuf", [128, 48], "bfloat16")
-        SCRATCH["e%s%d" % (_k, _i)] = ("sbuf", [128, 48], "float32")
-        for _c in (0, 1):
-            SCRATCH["g%s%d%d" % (_k, _i, _c)] = ("sbuf", [128, 384], "float32")
-            if _k == "h" or _i > 1:
-                SCRATCH["l%s%d%d" % (_k, _i, _c)] = ("sbuf", [128, 24], "uint16")
+declare("sbuf", "float32", H=HW, AR=AW, RA=48, MU=128, MQ=16, MX=24, RST=32, OF=4, KF=4, TF=4, XF=4, SC=32, LL=512, RR=192,
+        SND=48, RB=48, WW=16, SW=320, EYE=128, X0=384, XT0=384, QM=48, MM=48, SV=48, TH=48, TV=48, ANS=48,
+        Y0=256, Y1=256, TLF=1280, CF=24, I160=160, PF=8)
+declare("sbuf", "int32", RK=4, RT=4, KI=4, PI=2, TLI=1280)
+declare("sbuf", "bfloat16", C96=32, C15=32, ZB=128, LTI=128, LTB=128, TWO=128, OH=56, EYB=128, SWB=320, CL=48, C2=48, C3=48)
+declare("sbuf", "uint16", U0=4, U1=4, OFW=32, L0=24, LST0=16, LST1=16, LST2=16, AL0=16, AL1=16, AL2=16)
+declare("psum", "float32", p0=512, p1=512, p2=512, p3=512, p4=512, pV=512, pm0=512)
+SCRATCH["pm1"] = ("psum", [128, 32, 16], "float32")
+for _s in ("h1", "h2", "h3", "a1", "a2", "a3", "a4"):
+    SCRATCH["X" + _s] = ("sbuf", [128, NS, 272], "float32")
+    SCRATCH["G" + _s] = ("sbuf", [128, 768], "float32")
+    SCRATCH["h" + _s] = ("sbuf", [128, 48], "bfloat16")
+    SCRATCH["e" + _s] = ("sbuf", [128, 48], "float32")
+    if _s != "a1":
+        SCRATCH["l" + _s] = ("sbuf", [128, 48], "uint16")
+SCRATCH["TE"] = ("sbuf", [128, NS, 2 * W], "float32")
+SCRATCH["AF"] = ("dram", [2, 8, A], "float32")
 SCRATCH["OD"] = ("dram", [2, 128, 4], "uint16")
-SEMAPHORES = ["v", "s", "t", "gp", "ldk", "ldt", "thd", "tvp", "tvt", "tar", "ldh", "ldi", "lda", "ownk", "ownt", "od", "ow",
-              "rK0", "rK1", "rB", "lB", "rN0", "rN1", "rT", "rF", "ownf", "wa0", "wa1", "st0", "st1"]
+SEMAPHORES = ["v", "s", "t", "gp", "ldk", "ldt", "thd", "tvp", "tvt", "cast", "go", "ldh", "ldi", "lda", "od", "ow",
+              "rK0", "rK1", "rK2", "lB", "rN0", "rN1", "rN2", "rT", "rC", "rV", "rF", "ownf", "wa0", "wa1", "st0", "st1"]
 
 
 def readers(topo, cores, q):
     chips = [topo.chip(c) for c in cores]
-    after = [chips[(q + k) % N] for k in range(1, N) if chips[(q + k) % N] != chips[q]][0]
-    one = [r for r in range(N) if chips[r] not in (chips[q], after)]
-    return one + [r for r in range(N) if r not in one]
+    ring = [c for i, c in enumerate(chips) if c not in chips[:i]]
+    at = [[r for r in range(N) if chips[r] == ring[(ring.index(chips[q]) + d) % len(ring)]] for d in range(len(ring))]
+    mate = [r for r in at[0] if r != q]
+    if chips[(q + 1) % N] == chips[q]:
+        return at[1] + [q] + at[2] + mate + at[3]
+    return at[2] + [q] + mate + at[1] + at[3]
 
 
 def deal(topo, cores, me, dests):
@@ -57,11 +70,12 @@ def deal(topo, cores, me, dests):
 
 
 def asks(topo, cores, r, s):
-    return deal(topo, cores, r, [q for q in range(N) if q != r and readers(topo, cores, q).index(r) // 4 == s])
+    return deal(topo, cores, r, [q for q in range(N) if q != r and 3 * readers(topo, cores, q).index(r) // W == s])
 
 
 def tells(topo, cores, z, s):
-    return deal(topo, cores, z, [r for r in readers(topo, cores, (z - 1) % N)[4 * s:4 * s + 4] if r != z])
+    return deal(topo, cores, z, [r for k, r in enumerate(readers(topo, cores, (z - 1) % N))
+                                 if r != z and (3 * k + 2) // W == s])
 
 
 def bits(es):
@@ -125,14 +139,17 @@ def rank_program(g, core, T, topo):
         need(name, toks)
         return done(q[name].dma_start(out, src), sem, 16)
 
-    def swap(out, src, mat, start, stop, *toks, lo=0, hi=48):
+    def swap(out, src, mat, start, *toks, lo=0, hi=48, stop=False, view=None, into=None):
         tk = None
         for gs in range(2):
             for G in range(2):
-                k = 256 * gs + 128 * G
-                tk = mm(out[:, lo + gs:hi:2], mat[:, k:k + 128], src[:, lo + G:hi:2], start and gs + G == 0,
-                        stop and gs + G == 2, *toks)
+                k = 160 * gs + 16 - 16 * (G - gs)
+                tk = mm(into(gs) if into else out[:, lo + gs:hi:2], mat[:, k:k + 128], view(G) if view else src[:, lo + G:hi:2],
+                        start and gs + G == 0, stop and gs + G == 2, *toks)
         return tk
+
+    def same(out, src, mat, start, *toks, stop=False):
+        return mm(out[:, 0:48], mat[:, :], src[:, 0:48], start, stop, *toks)
 
     def iota(out, pat, base, cm, **kw):
         return done(g.iota(out, pat, base, cm, **kw), "gp", 1)
@@ -144,81 +161,97 @@ def rank_program(g, core, T, topo):
     fl = {"allow_small_or_imprecise_dtypes": True}
     k_rk = dma("y", T.RK[:, :], T.rk[:, :], "ldk")
     k_rt = dma("s", T.RT[:, :], T.rt[:, :], "ldt")
-    CH = 2048
-    tiles = {"hd": (0, K), "vp": (256, V), "vt": (768, V), "ap": (1280, A), "at": (1536, A)}
-    pieces = [(0, K), (K, K + CH), (K + CH, V)]
+    tiles = {"hd": (0, K), "vp": (256, V), "vt": (768, V)}
 
-    def tile(buf, name, lo, hi, cl):
+    def tile(buf, name, lo, hi, cl=None):
         c0, n = tiles[name]
         p0, h = 128 * lo // n, 64 * (hi - lo) // n
+        if cl is None:
+            return buf[p0:p0 + 2 * h, c0:c0 + n // 16]
         return buf[p0 + h * cl:p0 + h * cl + h, c0:c0 + n // 16]
 
-    def fetch(queue, name, sem):
-        for lo, hi in pieces:
-            for cl in range(2 if hi <= tiles[name][1] else 0):
-                k = dma(queue, tile(T.TLI, name, lo, hi, cl), T[name][cl:8:2, lo:hi], sem)
+    def fetch(name):
+        for lo, hi in PIECES[:1] if name == "hd" else PIECES:
+            k = dma("y", tile(T.TLI, name, lo, hi), T[name][:, lo:hi], "t" + name)
         return k
 
-    k_tl = {name: fetch("y", name, "t" + name) for name in ("hd", "vp", "vt")}
+    k_tl = {name: fetch(name) for name in ("hd", "vp", "vt")}
     z0 = fill(T.ZB[:, :], 0.0)
-    f0 = fill(T.ZF[:, :], 0.0)
-    i_m = iota(T.M32[:, :], [[0, 4], [1, 32]], 0, 0, **fl)
-    pick(T.LTI[:, :], T.ZB[:, :], [[-1, 128]], GE, 1.0, 0, 1, z0)
-    pick(T.EYB[:, :], T.ZB[:, :], [[1, 128]], NE, -BIG, 0, -1)
+    src0 = fill(T.H[:, V - 256:HW], 0.0)
+    src1 = fill(T.H[:, V - SRC:V - 256], 0.0)
+    i_q = iota(T.MQ[:, 8:16], [[4096, 8]], 0, 0, **fl)
+    w = pick(T.LTI[:, :], T.ZB[:, :], [[-1, 128]], GE, 2.0, 0, 1, z0)
     i_c = iota(T.C96[:, :], [[0, 4], [96, 8]], 0, 0, **fl)
-    G0, G1, V0, S2, V1 = 3456, 5632, 768, 4864, 7168
-    i_h = iota(T.H[:, G0:K], [[0, K - G0]], 0, 0, **fl)
-    i_g = iota(T.H[:, G1:3 * CH], [[0, 3 * CH - G1]], 0, 0, **fl)
+    i_l = pick(T.LTB[:, :], T.LTI[:, :], [[1, 128]], NE, -BIG, 0, -1, w)
+    i_m = iota(T.MU[:, :], [[0, 4], [2, 32]], -31, 0, **fl)
 
-    z1 = fill(T.ONE[:, :], 1.0)
+    def shares(who):
+        out, lo = [], 0
+        for e, n in FILL:
+            if e == who:
+                out.append((lo, lo + n))
+            lo += n
+        return out
+
+    filled = []
+    for lo, hi in shares("g"):
+        filled.append((lo, hi, iota(T.H[:, lo:hi], [[0, hi - lo]], 0, 0, **fl)))
+    iota(T.I160[:, :], [[1, 160]], 0, 0, **fl)
+    iota(T.PF[:, 0:2], [[1000, 2]], 16, 1, **fl)
+    i_p = iota(T.PI[:, 0:1], [[1, 1]], 0, 1)
+
+    fill(T.TWO[:, :], 2.0)
+    fill(T.C15[:, :], -15.5)
     z2 = fill(T.OH[:, 0:24], 0.0)
     w = fill(T.RST[:, :], 1.0)
-    f1 = fill(T.H[:, 0:V0], 0.0)
+    k_cf = fill(T.CF[:, 16:24], BIG)
     fill(T.RST[:, 0:32:8], 0.0, w)
+    k_mq = ts(T.MQ[:, 0:8], T.MQ[:, 8:16], M4096, None, ADD, None, i_q)
+    for lo, hi in shares("v"):
+        filled.append((lo, hi, fill(T.H[:, lo:hi], 0.0)))
 
-    def sfill(lo, hi, *toks):
-        for a0 in range(lo, hi, 256):
-            n = min(256, hi - a0)
-            k = act(T.H[:, a0:a0 + n], T.ZF[:, 0:n], *toks)
+    def sfill(lo, hi):
+        while lo < hi:
+            n = min(SRC if cnt.get("s") else 256, hi - lo)
+            k = act(T.H[:, lo:lo + n], T.H[:, V - n:V], src1 if cnt.get("s") else src0)
+            lo += n
         return k
 
     def convert(name):
         c0, n = tiles[name]
         return act(T.TLF[:, c0:c0 + n // 16], T.TLI[:, c0:c0 + n // 16], k_tl[name], bias=0.0 if name == "vt" else -float(V))
 
-    s_f = [sfill(V0, CH, f0), sfill(CH, G0)]
-    s_c = {name: convert(name) for name in ("hd", "vp", "vt")}
-    s_f += [sfill(K, S2), sfill(3 * CH, V1)]
+    s_c = {}
+    for i, (lo, hi) in enumerate(shares("s")):
+        filled.append((lo, hi, sfill(lo, hi)))
+        for name in CONVERT[i]:
+            s_c[name] = convert(name)
+    filled.append((V - SRC, V, filled[-1][2]))
 
-    w = ts(T.OI[:, :], T.RK[:, :], 12, None, SHR, None, k_rk)
-    k_of = cp(T.OF[:, :], T.OI[:, :], w)
-    for f in range(4):
-        k_oh = ts(T.OH[:, 24 + 8 * f:32 + 8 * f], T.M32[:, 0:8], T.OF[:, f:f + 1], None, EQ, None, k_of, z2, i_m)
-    mm(T.p0[:, 0:32], T.ONE[0:1, :], T.C96[0:1, :], True, False, z1, i_c)
-    mm(T.p0[:, 0:32], T.LTI[:, :], T.OH[:, 24:56], False, False, k_oh)
-    mm(T.p0[:, 0:32], T.EYB[:, :], T.OH[:, 24:56], False, False)
-    for d in (1, 2, 3):
-        m = mm(T.p0[:, 0:32], T.ONE[:, :], T.OH[:, 24 - 8 * d:56 - 8 * d], False, d == 3)
+    k_of = ts(T.OF[:, :], T.RK[:, :], -2047.5, M4096, ADD, ADD, k_rk)
     w = ts(T.KI[:, :], T.RK[:, :], 4095, None, AND, None)
-    k_tf = ts(T.TF[:, :], T.RT[:, :], 1.0, None, ADD, None, k_rt)
-    k_kf = cp(T.KF[:, :], T.KI[:, :], w)
+    mm(T.p0[:, 0:32], T.TWO[0:1, :], T.C96[0:1, :], True, False, z2, i_c)
+    mm(T.p0[:, 0:32], T.TWO[0:1, :], T.C15[0:1, :], False, False)
+    for f in range(4):
+        k = ts(T.OH[:, 24 + 8 * f:32 + 8 * f], T.MQ[:, 0:8], T.OF[:, f:f + 1], None, EQ, None, k_of, k_mq)
+        m = mm(T.p0[:, 0:32], (T.LTB if f == 3 else T.TWO)[:, :], T.OH[:, 8 * f:32 + 8 * f], False, f == 3, k, i_l)
+    ts(T.TF[:, :], T.RT[:, :], 1.0, None, ADD, None, k_rt)
+    cp(T.KF[:, :], T.KI[:, :], w)
     need("v", [m])
     w = done(g.vector.tensor_tensor_scan(T.SC[:, :], T.RST[:, :], T.p0[:, 0:32], 0.0, MUL, MIN), "v", 1)
-    ts(T.UI[:, 0:4], T.SC[:, 7:32:8], 31, None, AND, None, w)
-    w = ts(T.UI[:, 4:8], T.SC[:, 7:32:8], 5, 31, SHR, AND)
-    k_uf = cp(T.UF[:, :], T.UI[:, :], w)
+    ts(T.MX[:, :], T.MU[:, 0:24], 32.0, 992.0 - BIG, MUL, ADD, i_m)
+    k_xf = ts(T.XF[:, :], T.SC[:, 7:32:8], M64, M64, ADD, SUB, w)
     for f in range(4):
         for j, val in enumerate((T.KF, T.TF)):
-            ts(T.RR[:, 48 * f + j:48 * f + 48:2], T.M32[:, 0:24], T.UF[:, 4 + f:5 + f], val[:, f:f + 1], EQ, MUL, k_uf)
-        w = ts(T.LL[:, 128 * f:128 * f + 128], T.M32[:, :], T.UF[:, f:f + 1], None, EQ, None)
+            ts(T.RR[:, 48 * f + j:48 * f + 48:2], T.MX[:, :], T.XF[:, f:f + 1], val[:, f:f + 1], EQ, MUL, k_xf)
+        w = ts(T.LL[:, 128 * f:128 * f + 128], T.MU[:, :], T.XF[:, f:f + 1], T.SC[:, 8 * f + 7:8 * f + 8], ADD, EQ)
         m = mm(T.p1[:, 0:48], T.LL[:, 128 * f:128 * f + 128], T.RR[:, 48 * f:48 * f + 48], f == 0, f == 3, w)
-    fill(T.H[:, S2:S2 + 256], 0.0)
     k_snd = cp(T.SND[:, :], T.p1[:, 0:48], m)
-    f3 = fill(T.H[:, S2 + 256:G1], 0.0)
-    f2 = fill(T.H[:, V1:HW], 0.0)
+    for lo, hi in shares("w"):
+        filled.append((lo, hi, fill(T.H[:, lo:hi], 0.0)))
+    cp(T.L0[:, 6:9], T.SND[:, 6 * me:6 * me + 6:2], k_snd)
     fill(T.CF[:, 8:16], float(A))
-    fill(T.CF[:, 16:24], BIG)
-    k_cf = fill(T.AR[:, A:AW], 0.0)
+    k_ca = fill(T.AR[:, A:AW], 0.0)
 
     sent = [0]
 
@@ -239,143 +272,163 @@ def rank_program(g, core, T, topo):
         k = readers(topo, cores, q).index(r)
         return buf[:, 6 * k:6 * k + 6]
 
-    for s in range(2):
+    def ask(s):
         spread(asks(topo, cores, me, s), lambda d: T.SND[:, 6 * d:6 * d + 6], lambda d: slot(T.RB, d, me), "rK%d" % s, k_snd)
-    r_k = [("rK%d" % s, arrivals(asks, [s])) for s in range(2)]
-    r_f = ("rF", arrivals(tells, [0, 1]))
 
-    k_eye = pick(T.EYE[:, :], T.ZF[:, 0:128], [[1, 128]], NE, 1.0, 0, -1, f0)
-    for mat, zero, val in ((T.SW, T.ZF, 1.0), (T.SWB, T.ZB, -BIG)):
-        for gs in range(2):
-            for G in range(2):
-                k = 256 * gs + 128 * G
-                k_swb = pick(mat[:, k:k + 128], zero[:, 0:128], [[32, 4], [1016, 2], [1, 16]], NE, val,
-                             -1000 * G - 16 * (G - gs), -1)
-        if val > 0:
-            k_sw = k_swb
+    ask(0)
+    ask(1)
+    r_k = [("rK%d" % s, arrivals(asks, [s])) for s in range(NS)]
+    r_f = ("rF", arrivals(tells, range(NS)))
 
-    def rows(lo, hi, src, row, sem, *toks):
+    w = ts(T.PI[:, 1:2], T.PI[:, 0:1], 16, None, AND, None, i_p)
+    ts(T.EYE[:, :], T.I160[:, 16:144], T.PF[:, 0:1], None, EQ, None)
+    w = cp(T.PF[:, 2:3], T.PI[:, 1:2], w)
+    ts(T.PF[:, 3:4], T.PF[:, 2:3], 62.5, T.PF[:, 0:1], MUL, ADD, w)
+    w = ts(T.PF[:, 4:5], T.PF[:, 2:3], -62.5, T.PF[:, 1:2], MUL, ADD)
+    for gs in range(2):
+        k_mat = ts(T.SW[:, 160 * gs:160 * gs + 160], T.I160[:, :], T.PF[:, 3 + gs:4 + gs], None, EQ, None, w)
+
+    def scaled(out, mat):
+        return ts(out, mat, -BIG, None, MUL, None, k_mat)
+
+    def rows(win, lo, hi, src, row, sem, *toks):
         for gam in range(2):
             for cl in range(2):
-                k = dma("y", win[16 * gam + row + 8 * cl:128:32, lo:hi], src(cl), sem, *toks)
+                k = dma("s" if gam and hi == V else "y", win[16 * gam + row + 8 * cl:128:32, lo:hi], src(cl), sem, *toks)
         return k
 
-    win = T.H
-
     def cols(t, lo, hi):
-        return lambda cl: t[cl:8:2, lo:hi]
+        return lambda cl: t[4 * cl:4 * cl + 4, lo:hi]
 
-    def table(name, lo, hi, sem, *toks):
-        return rows(lo, hi, lambda cl: tile(T.TLF, name, lo, hi, cl), place[name], sem, *toks)
-
-    place = {"hd": RHD, "vp": RVP, "vt": RVT, "ap": RVP, "at": RVT}
-    for i, toks in enumerate(([f1], [i_h], [i_g, f3], [f2])):
-        sem = "ldh" if i < 2 else "ldi"
-        rows(CH * i, CH * i + CH, cols(T.vv, CH * i, CH * i + CH), RVV, sem, s_f[i], *toks)
-        for name in ([], ["hd", "vp", "vt"], ["vp", "vt"], ["vp", "vt"])[i]:
-            k = table(name, *pieces[i - 1], sem, s_c[name])
-        if i == 1:
+    place = {"hd": RHD, "vp": RVP, "vt": RVT}
+    for name, lo, hi in LOADS:
+        sem = "ldh" if lo < K else "ldi"
+        toks = [k for a, b, k in filled if a < hi and lo < b]
+        if name == "copies":
+            for r in range(RHD + 1, 8):
+                k = dma("y", T.H[r:128:8, lo:hi], T.vv[:, 0:2 * (hi - lo)], sem)
+        elif name == "vv":
+            k = rows(T.H, lo, hi, cols(T.vv, lo, hi), RVV, sem, *toks)
+        elif name == "end":
+            k = dma("y", T.H[RVT:128:8, lo:hi], T.CF[0:16, 16:24], sem, k_cf)
+        else:
+            k = rows(T.H, lo, hi, lambda cl: tile(T.TLF, name, lo, hi, cl), place[name], sem, s_c[name], *toks)
+        if lo < K:
             k_h0 = k
-            k_own = dma("y", slot(T.RB, me, me), T.SND[:, 6 * me:6 * me + 6], "ownk", k_snd)
-        if i == 0:
-            fetch("y", "ap", "tar")
-            c_ar = act(T.TLF[:, 1280:1792], T.TLI[:, 1280:1792], fetch("y", "at", "tar"))
-    k_h = dma("y", T.H[RVT:128:8, V:HW], T.CF[0:16, 16:24], "ldi", k_cf)
-    win = T.AR
-    rows(0, A, cols(T.av, 0, A), RVV, "lda")
+    k_h = k
+    g.sync.sem_inc(T.sem.go, 1)
+    g.scalar.sem_inc(T.sem.go, 1)
+    need("g", [("go", 2)])
+    ask(2)
+    dma("g", T.AF[0], T.ap[:, :], "cast")
+    k_cast = dma("g", T.AF[1], T.at[:, :], "cast")
+    dma("y", T.AR[RVP:128:8, A:AW], T.CF[0:16, 8:16], "lda", k_ca)
+    dma("y", T.AR[RVT:128:8, A:AW], T.CF[0:16, 16:24], "lda")
+    need("y", [r_k[0]])
     for r in range(RVV + 1, 8):
         dma("y", T.AR[r:128:8, 0:A], T.vv[:, :], "lda")
-    dma("y", T.AR[RVP:128:8, A:AW], T.CF[0:16, 8:16], "lda")
-    dma("y", T.AR[RVT:128:8, A:AW], T.CF[0:16, 16:24], "lda")
-    table("ap", 0, A, "lda", c_ar)
-    k_ar = table("at", 0, A, "lda")
+    rows(T.AR, 0, A, cols(T.av, 0, A), RVV, "lda")
+    rows(T.AR, 0, A, lambda cl: T.AF[0, 4 * cl:4 * cl + 4, :], RVP, "lda", k_cast)
+    k_ar = rows(T.AR, 0, A, lambda cl: T.AF[1, 4 * cl:4 * cl + 4, :], RVT, "lda")
 
-    def row(x, r, cl=None):
-        a = 8 + r + (384 * cl if cl else 0)
-        return x[:, a:a + (753 if cl is None else 369):16]
+    def span(j, c=None):
+        if j is None:
+            return 0, 48
+        return (16 * j, 16 * j + 16) if c is None else (16 * j + 8 * c, 16 * j + 8 * c + 8)
 
-    def both(x, cl):
-        return x[:, 24 * cl:24 * cl + 24]
+    def row(step, r, j=None, c=None):
+        lo, hi = span(0, c)
+        cut = slice(8 + r + 16 * lo, 8 + r + 16 * hi - 15, 16)
+        return T["X" + step][:, :, cut] if j is None else T["X" + step][:, j, cut]
 
-    def part(x, s, c):
-        return x[:, 24 * s + 12 * c:24 * s + 12 * c + 12]
+    def part(x, j=None, c=None):
+        lo, hi = span(j, c)
+        return x[:, lo:hi]
 
-    def hd_row(s, c):
-        a = 192 * s + RHD + 8 * (1 - c)
-        return T.XT0[:, a:a + 177:16]
+    got = {}
 
-    lst, got = [], []
-    for s in range(2):
-        lo = 12 * s
-        w = cp(T.L0[:, lo:lo + 12], T.RB[:, 2 * lo:2 * lo + 24:2], r_k[s], *([k_own] if s else []))
-        if s == 0:
-            got = [act(T.X0[:, 96:192], T.H[:, 0:K].indirect(T.L0[:, 6:12]), w, k_h0)]
-            got.append(cp(T.X0[:, 0:96], T.H[:, 0:K].indirect(T.L0[:, 0:6]), w, k_h0))
-        else:
-            cp(part(T.TE, 0, 0), T.RB[:, 1:24:2])
-            got = [cp(T.X0[:, 192:384], T.H[:, 0:K].indirect(T.L0[:, 12:24]), w)]
-            cp(part(T.TE, 0, 1), T.RB[:, 1:24:2])
-        w = tr(T.XT0[:, 192 * s:192 * s + 192], T.X0[:, 192 * s:192 * s + 192], *got)
-        if s == 1:
-            cp(part(T.TE, 1, 0), T.RB[:, 25:48:2])
-        for c in range(2):
-            k = ts(T["lh1%d" % s][:, 12 * c:12 * c + 12], hd_row(s, c), float(V), float(V), ADD, MIN, w)
-        lst.append(k)
+    def gather(step, j, *toks, c=None):
+        lo, hi = span(j, c)
+        win = T.H[:, 0:HW] if step[0] == "h" else T.AR[:, 0:AW]
+        offs = T["AL%d" % j][:, :] if step == "a1" else T["l" + step][:, lo:hi]
+        k = act(T["G" + step][:, 16 * lo:16 * hi], win.indirect(offs), *toks)
+        for cc in range(2) if c is None else [c]:
+            got[step, j, cc] = k
 
-    X, first = {}, {"h": float(V), "a": 0.0}
+    def turn(step, j, c):
+        lo, hi = span(j, c)
+        return tr(T["X" + step][:, j, 136 * c:136 * c + 128], T["G" + step][:, 16 * lo:16 * hi], got[step, j, c])
 
-    def walk(kind, i, win, offs, toks, extra, after):
-        x = X[i] = T["X%s%d" % (kind, i)]
-        new, k = [], None
-        for cl in range(2):
-            buf = T["g%s%d%d" % (kind, i, cl)]
-            a = act(buf[:, :], win.indirect(offs[cl]), toks[cl], *extra)
-            o = 384 * cl
-            tr(x[:, o:o + 192], buf[:, 0:192], *([a] + ([k] if k else [])))
-            k = tr(x[:, o + 200:o + 392], buf[:, 192:384])
-            new.append(after(cl, x, k))
-        return new
+    def nextlist(step, then, j, k):
+        add, cap = (float(V), float(V)) if step[0] == "h" else (0.0, float(A))
+        k = ts(part(T["l" + then], j), row(step, RVP, j), add, cap, ADD, MIN, k)
+        for c in range(2) if (then, j) == ("a4", NS - 1) else [None]:
+            gather(then, j, k, c=c)
 
-    def offs(kind, i):
-        return [T["l%s%d%d" % (kind, i, cl)][:, 0:24] for cl in range(2)]
+    def stops(step, open_t, *toks, j=None):
+        return tt(part(T["h" + step], j), row(step, RVT, j), part(open_t, j), LT, *toks)
 
-    def nextlist(kind, i, cl, x, k, cap):
-        return ts(T["l%s%d%d" % (kind, i + 1, cl)][:, :], row(x, RVP, cl), first[kind], cap, ADD, MIN, k)
+    def gives(step, *toks, j=None):
+        return tt(part(T["e" + step], j), part(T["h" + step], j), row(step, RVV, j), MUL, *toks)
 
-    def stops(kind, i, open_t, *toks):
-        return tt(T["h%s%d" % (kind, i)][:, :], row(X[i], RVT), open_t, LT, *toks)
-
-    def gives(kind, i, *toks):
-        return tt(T["e%s%d" % (kind, i)][:, :], T["h%s%d" % (kind, i)][:, :], row(X[i], RVV), MUL, *toks)
+    def walk(slots, then=None):
+        turn(slots[0][0], slots[0][1], 0)
+        for n, (step, j, after, fillers) in enumerate(slots):
+            k = turn(step, j, 1)
+            nx = slots[n + 1][:2] if n + 1 < len(slots) else then
+            if nx and step != "h3":
+                turn(nx[0], nx[1], 0)
+            for f in fillers:
+                f()
+            after(j, k)
+            if nx and step == "h3":
+                turn(nx[0], nx[1], 0)
 
     S = {}
-    win = T.H[:, 0:HW]
-    pm = (T.p5, T.p7)
 
-    def heap1(cl, x, k):
-        if cl == 0:
-            swap(T.p1, T.TE, T.SW, True, False, cp(part(T.TE, 1, 1), T.RB[:, 25:48:2]), k_sw)
-            mm(T.p2[:, 0:48], T.EYE[:, :], T.TE[:, :], True, False, k_eye)
-            mm(T.p3[:, 0:48], T.EYE[:, :], T.TE[:, :], True, False)
-        new = nextlist("h", 1, cl, x, k, float(V))
-        if cl == 1:
-            S["h"] = stops("h", 1, T.TE[:, :])
-            S["t2"] = swap(T.p1, T.hh1, T.SWB, False, True, S["h"], k_swb)
-            mm(T.p2[:, 0:48], T.EYB[:, :], T.hh1[:, :], False, False)
-            mm(T.p3[:, 0:48], T.EYB[:, :], T.hh1[:, :], False, False)
-        return new
+    def keys(j):
+        lo, hi = ((0, 6), (9, 16), (16, 24))[j]
+        return cp(T.L0[:, lo:hi], T.RB[:, 2 * lo:2 * hi:2], r_k[j])
 
-    def heap2(cl, x, k):
-        if cl == 0:
-            gives("h", 1, S["h"])
-        new = nextlist("h", 2, cl, x, k, float(V))
+    def first(j, k):
+        return act(T.X0[:, 128 * j:128 * j + 128], T.H[:, 0:K].indirect(T.L0[:, 8 * j:8 * j + 8]), k)
+
+    def turned(j, *toks):
+        return tr(T.XT0[:, 128 * j:128 * j + 128], T.X0[:, 128 * j:128 * j + 128], *toks)
+
+    def heads(j, w):
         for c in range(2):
-            a = 8 + RVP + 384 * cl + 192 * c
-            w = tt(part(T.QM, cl, c), hd_row(cl, c), x[:, a:a + 177:16], MAX)
-        if cl == 1:
-            S["mm0"] = tt(both(T.MM, 0), row(X[1], RVP, 0), both(pm[0], 0), MAX, S["pm0"])
-        S["pm%d" % cl] = swap(pm[cl], T.QM, T.SW, True, True, w, lo=24 * cl, hi=24 * cl + 24)
-        return new
+            a = 128 * j + RHD + 8 * (1 - c)
+            k = ts(part(T.lh1, j, c), T.XT0[:, a:a + 113:16], float(V), float(V), ADD, MIN, w)
+        for c in range(2 if j == NS - 1 else 0):
+            a = RHD + 8 * (1 - c)
+            S["t0"] = swap(None, None, T.SW, c == 0, w, k_mat, stop=c == 1, view=lambda G: T.XT0[:, a + 16 * G:a + 369:32],
+                           into=lambda gs: T.pm1[:, 0:NS, 8 * c + gs:8 * c + 8:2])
+        return k
+
+    k = keys(0)
+    w = turned(0, act(T.X0[:, 64:128], T.H[:, 0:K].indirect(T.L0[:, 4:8]), k, k_h0),
+               cp(T.X0[:, 0:64], T.H[:, 0:K].indirect(T.L0[:, 0:4]), k, k_h0))
+    f1 = first(1, keys(1))
+    gather("h1", 0, heads(0, w), k_h)
+    k_own = cp(T.RB[:, 13:18:2], T.SND[:, 6 * me + 1:6 * me + 6:2])
+    scaled(T.EYB[:, :], T.EYE[:, :])
+    w = turned(1, f1)
+    f2 = first(2, keys(2))
+    gather("h1", 1, heads(1, w))
+    scaled(T.SWB[:, 0:160], T.SW[:, 0:160])
+    turn("h1", 0, 0)
+    k = turn("h1", 0, 1)
+    w = turned(2, f2)
+    k = ts(part(T.lh2, 0), row("h1", RVP, 0), float(V), float(V), ADD, MIN, k)
+    gather("h1", 2, heads(2, w))
+    gather("h2", 0, k)
+    turn("h1", 1, 0)
+    k = turn("h1", 1, 1)
+    for c in range(2):
+        k_te = cp(T.TE[:, :, 8 * c:8 * c + 8], T.RB[:, 1:48:2], k_own)
+    nextlist("h1", "h2", 1, k)
+    scaled(T.SWB[:, 160:320], T.SW[:, 160:320])
 
     zc = cores[nxt]
     rid, pid, _ = topo.addr(zc)
@@ -388,111 +441,132 @@ def rank_program(g, core, T, topo):
         sent[0] += far_n
         return (rsem, far_n)
 
-    def heap3(cl, x, k):
-        if cl == 0:
-            S["h"] = stops("h", 2, T.p1[:, 0:48], S["t2"])
-            S["t3"] = swap(T.p2, T.hh2, T.SWB, False, True, S["h"])
-            swap(T.p3, T.hh2, T.SWB, False, False)
-            mm(T.p4[:, 0:48], T.EYE[:, :], T.eh1[:, :], True, False)
-        else:
-            S["v2"] = swap(T.p4, T.eh2, T.SW, False, True, gives("h", 2, S["h"]))
-        w = tt(T["LST%d" % cl][:, :], row(x, RVP, cl), both(T.MM, cl), MAX, k, S["mm%d" % cl])
-        if cl == 0:
-            S["mm1"] = tt(both(T.MM, 1), row(X[1], RVP, 1), both(pm[1], 1), MAX, S["pm1"])
-        else:
-            S["h"] = stops("h", 3, T.p2[:, 0:48], S["t3"])
-        return onward(T["AL%d" % cl][:, :], T["LST%d" % cl][:, :], "rN%d" % cl, w)
+    r_t = onward(T.TH[:, :], T.TE[:, :, :], "rT", k_te)
+    swap(T.p2, None, T.SW, True, k_te, view=lambda G: T.TE[:, :, G:16:2])
 
-    lst = walk("h", 1, win, offs("h", 1), lst, [k_h], heap1)
-    lst = walk("h", 2, win, offs("h", 2), lst, [], heap2)
-    r_n = walk("h", 3, win, offs("h", 3), lst, [], heap3)
-    k_t4 = mm(T.p3[:, 0:48], T.EYB[:, :], T.hh3[:, :], False, True, S["h"])
-    ke = gives("h", 3, S["h"])
-    cp(T.SD[:, 0:48], T.p3[:, 0:48], k_t4)
-    w = tt(T.SD[:, 48:96], T.eh3[:, :], T.p4[:, 0:48], ADD, ke, S["v2"])
-    r_t = onward(T.TH[:, :], T.SD[:, :], "rT", w)
-    ts(T.WW[:, 0:4], T.UF[:, 0:4], 48.0, None, MUL, None)
-    w = ts(T.WW[:, 4:8], T.UF[:, 4:8], 2.0, None, MUL, None)
-    w = tt(T.WW[:, 8:12], T.WW[:, 0:4], T.WW[:, 4:8], ADD, w)
-    ts(T.U0[:, :], T.WW[:, 8:12], 0.0, None, ADD, None, w)
-    k_u = ts(T.U1[:, :], T.WW[:, 8:12], 1.0, None, ADD, None)
+    def stops1():
+        k = tt(T.hh1[:, :], row("h1", RVT), T.TE[:, :, :], LT)
+        S["t2"] = swap(T.p2, T.hh1, T.SWB, False, k, stop=True)
+
+    def stops2():
+        mm(T.p3[:, 0:48], T.EYE[:, :], T.TE[:, :, :], True, False)
+        same(T.p3, T.hh1, T.EYB, False)
+        same(T.p4, T.hh1, T.EYB, True)
+        S["t3"] = swap(T.p3, T.hh2, T.SWB, False, stops("h2", T.p2, S["t2"]), stop=True)
+        S["t4"] = swap(T.p4, T.hh2, T.SWB, False, stop=True)
+
+    def closed():
+        ts(T.CL[:, :], T.p4[:, 0:48], -1.0 / BIG, None, MUL, None, S["t4"])
+
+    pm, r_n = {1: (T.pm0, 0, 2), 2: (T.p0, 2, 3)}, []
+
+    def larger():
+        S["qm"] = tt(T.QM[:, :], row("h1", RVP), T.pm1[:, 0:NS, :], MAX, S["t0"])
+
+    def second(j, k):
+        if j in pm:
+            bank, lo, hi = pm[j]
+            S["pm", j] = swap(bank, None, T.SW, True, k, lo=16 * lo, hi=16 * hi, stop=True,
+                              view=lambda G: T.Xh2[:, lo:hi, 8 + RVP + 16 * G:8 + RVP + 241:32])
+        nextlist("h2", "h3", j, k)
+
+    def largest(j):
+        def call():
+            bank, lo, hi = pm[j]
+            k = tt(T.MM[:, 16 * lo:16 * hi], T.QM[:, 16 * lo:16 * hi], bank[:, 16 * lo:16 * hi], MAX, S["pm", j], S["qm"])
+            for i in range(lo, hi):
+                S["mm", i] = k
+        return call
+
+    def leave(j, k):
+        w = tt(T["LST%d" % j][:, :], row("h3", RVP, j), part(T.MM, j), MAX, k, S["mm", j])
+        r_n.append(onward(T["AL%d" % j][:, :], T["LST%d" % j][:, :], "rN%d" % j, w))
+
+    walk([("h1", 2, lambda j, k: nextlist("h1", "h2", j, k), []),
+          ("h2", 0, second, [stops1]), ("h2", 1, second, []), ("h2", 2, second, [larger]),
+          ("h3", 0, leave, [largest(1), stops2]), ("h3", 1, leave, [largest(2)]), ("h3", 2, leave, [closed])])
+    k_h3 = stops("h3", T.p3, S["t3"])
+    gives("h1")
+    r_c = onward(T.C3[:, :], T.C2[:, :], "rC", tt(T.C2[:, :], T.CL[:, :], T.hh3[:, :], MAX, k_h3))
+    swap(T.pV, T.eh2, T.SW, True, gives("h2"))
+    t_v = same(T.pV, T.eh1, T.EYE, False, stop=True)
+    gives("h3")
+    w = tt(T.WW[:, 0:4], T.SC[:, 7:32:8], T.XF[:, :], SUB)
+    ts(T.WW[:, 4:8], T.XF[:, :], BIG, 1.0 / 32, ADD, MUL)
+    w = ts(T.WW[:, 8:12], T.WW[:, 0:4], 31.0, 24.0, ADD, MUL, w)
+    w = tt(T.WW[:, 12:16], T.WW[:, 4:8], T.WW[:, 8:12], ADD, w)
+    ts(T.U0[:, :], T.WW[:, 12:16], 0.0, None, ADD, None, w)
+    k_u = ts(T.U1[:, :], T.WW[:, 12:16], 1.0, None, ADD, None)
+    r_v = onward(T.TV[:, :], T.SV[:, :], "rV", tt(T.SV[:, :], T.eh3[:, :], T.pV[:, 0:48], ADD, t_v))
     dma("y", T.OD[0], T.U0[:, :], "od", k_u)
     k_od = dma("y", T.OD[1], T.U1[:, :], "od")
     for gr in range(8):
-        k_ow = dma("y", T.OFW[16 * gr:16 * gr + 16, :], T.OD[gr % 2], "ow", k_od)
+        k_ow = dma("y", T.OFW[16 * gr:16 * gr + 16, :], T.OD[gr // 4], "ow", k_od)
 
-    win = T.AR[:, 0:AW]
-    k_t1 = swap(T.p1, T.TH, T.SW, True, True, r_t, k_u)
-    mm(T.p2[:, 0:48], T.EYE[:, :], T.TH[:, 0:48], True, False)
+    for src, one, other, tok in ((T.TH, T.EYE, T.SW, r_t), (T.C3, T.EYB, T.SWB, r_c)):
+        t_1 = swap(T.p1, src, other, src is T.TH, tok, k_h3, stop=src is T.C3)
+        same(T.p2, src, one, src is T.TH)
+        swap(T.p3, src, other, src is T.TH)
+        same(T.p4, src, one, src is T.TH)
 
-    def arch1(cl, x, k):
-        return nextlist("a", 1, cl, x, k, float(A))
+    def a_stops1():
+        S["h1"] = stops("a1", T.p1, t_1)
+        S["t2"] = swap(T.p2, T.ha1, T.SWB, False, S["h1"], stop=True)
+        same(T.p3, T.ha1, T.EYB, False)
+        swap(T.p4, T.ha1, T.SWB, False)
 
-    def arch2(cl, x, k):
-        if cl == 0:
-            S["h"] = stops("a", 1, T.p1[:, 0:48], k_t1)
-            S["t2"] = swap(T.p2, T.ha1, T.SWB, False, True, S["h"])
-            mm(T.p3[:, 0:48], T.EYB[:, :], T.ha1[:, :], True, False)
-            swap(T.p3, T.TH, T.SW, False, False)
-        new = nextlist("a", 2, cl, x, k, float(A))
-        if cl == 0:
-            gives("a", 1, S["h"])
-        else:
-            S["h"] = stops("a", 2, T.p2[:, 0:48], S["t2"])
-            S["t3"] = swap(T.p3, T.ha2, T.SWB, False, True, S["h"])
-            mm(T.p4[:, 0:48], T.EYB[:, :], T.ha2[:, :], True, False)
-            swap(T.p4, T.ha1, T.SWB, False, False)
-            mm(T.p4[:, 0:48], T.EYE[:, :], T.TH[:, 0:48], False, False)
-            mm(T.p6[:, 0:48], T.EYE[:, :], T.TH[:, 48:96], True, False)
-            swap(T.p6, T.ea1, T.SW, False, False)
-        return new
+    def a_gives1():
+        swap(T.pV, T.ea1, T.SW, True, gives("a1", S["h1"]))
 
-    def arch3(cl, x, k):
-        if cl == 0:
-            mm(T.p6[:, 0:48], T.EYE[:, :], T.ea2[:, :], False, False, gives("a", 2, S["h"]))
-        new = nextlist("a", 3, cl, x, k, float(A))
-        if cl == 1:
-            S["h"] = stops("a", 3, T.p3[:, 0:48], S["t3"])
-            S["t4"] = swap(T.p4, T.ha3, T.SWB, False, True, S["h"])
-            S["sum"] = swap(T.p6, T.ea3, T.SW, False, True, gives("a", 3, S["h"]))
-        return new
+    def a_stops2():
+        S["h2"] = stops("a2", T.p2, S["t2"])
+        S["t3"] = swap(T.p3, T.ha2, T.SWB, False, S["h2"], stop=True)
+        same(T.p4, T.ha2, T.EYB, False)
 
-    lst = walk("a", 1, win, [T.AL0[:, :], T.AL1[:, :]], r_n, [k_ar], arch1)
-    lst = walk("a", 2, win, offs("a", 2), lst, [], arch2)
-    lst = walk("a", 3, win, offs("a", 3), lst, [], arch3)
+    def a_gives2():
+        same(T.pV, T.ea2, T.EYE, False, gives("a2", S["h2"]))
+        same(T.pV, T.TV, T.EYE, False, r_v)
 
-    x = T.Xa4
+    for j in range(NS):
+        gather("a1", j, r_n[j], k_ar)
+    fillers = {("a2", 1): [a_stops1], ("a2", 2): [a_gives1], ("a3", 0): [a_stops2], ("a3", 1): [a_gives2]}
+    walk([(step, j, lambda j, k, step=step, then=then: nextlist(step, then, j, k), fillers.get((step, j), []))
+          for step, then in (("a1", "a2"), ("a2", "a3"), ("a3", "a4")) for j in range(NS)], then=("a4", 0))
+    h3 = stops("a3", T.p3, S["t3"])
+    t_4 = swap(T.p4, T.ha3, T.SWB, False, h3, stop=True)
 
-    def hit(s, *toks):
-        return tt(both(T.ha4, s), row(x, RVT, s), both(T.p4, s), LT, S["t4"], *toks)
+    def answer(j, c, *toks):
+        return tt(T.ANS[:, 16 * j + 1 - c:16 * j + 16:2], part(T.ea4, j, c), part(T.pV, j, c), ADD, t_v, *toks)
 
-    def value(s, *toks):
-        return tt(both(T.ea4, s), both(T.ha4, s), row(x, RVV, s), MUL, *toks)
+    def tell(j, k):
+        spread(tells(topo, cores, me, j), lambda d: slot(T.ANS, prv, d), lambda d: T.RA[:, 6 * prv:6 * prv + 6], "rF", k)
 
-    def tell(s, *toks):
-        for c in range(2):
-            k = tt(T.ANS[:, 24 * s + 1 - c:24 * s + 24:2], part(T.ea4, s, c), part(T.p6, s, c), ADD, S["sum"], *toks)
-        spread(tells(topo, cores, me, s), lambda d: slot(T.ANS, prv, d), lambda d: T.RA[:, 6 * prv:6 * prv + 6], "rF", k)
-        return k
-
-    a0 = act(T.ga40[:, :], win.indirect(T.la40[:, :]), lst[0])
-    a1 = act(T.ga41[:, 0:192], win.indirect(T.la41[:, 0:12]), lst[1])
-    a2 = act(T.ga41[:, 192:384], win.indirect(T.la41[:, 12:24]))
-    tr(x[:, 0:192], T.ga40[:, 0:192], a0)
-    w = hit(0, tr(x[:, 200:392], T.ga40[:, 192:384]))
-    tr(x[:, 384:576], T.ga41[:, 0:192], a1)
-    w = value(0, w)
-    k = tr(x[:, 584:776], T.ga41[:, 192:384], a2)
-    tell(0, w)
-    k_ans = tell(1, value(1, hit(1, k)))
+    k = turn("a4", 0, 1)
+    t_v = swap(T.pV, T.ea3, T.SW, False, gives("a3", h3), stop=True)
+    turn("a4", 1, 0)
+    h0 = stops("a4", T.p4, t_4, k, j=0)
+    k = turn("a4", 1, 1)
+    e0 = gives("a4", h0, j=0)
+    turn("a4", 2, 0)
+    h1 = stops("a4", T.p4, k, j=1)
+    k = turn("a4", 2, 1)
+    e1 = gives("a4", h1, j=1)
+    answer(0, 0, e0)
+    tell(0, answer(0, 1))
+    h2 = stops("a4", T.p4, k, j=2)
+    answer(1, 0, e1)
+    tell(1, answer(1, 1))
+    answer(2, 0, gives("a4", h2, j=2))
+    k_ans = answer(2, 1)
+    tell(2, k_ans)
 
     k_of2 = dma("y", T.RA[:, 6 * prv:6 * prv + 6], slot(T.ANS, prv, me), "ownf", k_ans)
     ends = []
     for cl, nm in ((0, "y"), (1, "s")):
-        ends.append(dma(nm, T.H[16 * cl:128:32, 0:1536], T.RA[:, :], "wa%d" % cl, r_f, k_of2))
+        ends.append(dma(nm, T.H[64 * cl:64 * cl + 64:16, 0:1536], T.RA[:, :], "wa%d" % cl, r_f, k_of2))
     need("v", ends + [k_ow])
     yv = done(g.vector.tensor_copy(T.Y0[:, :], T.H[:, 0:1536].indirect(T.OFW[:, 0:16])), "v", 1)
     ys = act(T.Y1[:, :], T.H[:, 0:1536].indirect(T.OFW[:, 16:32]), *(ends + [k_ow]))
     dma("y", T.y[:, 0:256], T.Y0[0:128:16, :], "st0", yv)
     dma("s", T.y[:, 256:512], T.Y1[0:128:16, :], "st1", ys)
-    need("g", [("lB", sent[0]), r_n[0], r_n[1], r_t, r_f] + r_k + list(cnt.items()))
+    need("g", [("lB", sent[0]), r_t, r_c, r_v, r_f] + r_n + r_k + list(cnt.items()))

from concourse.bass import DstId, RemoteDMATransfer
from concourse.mybir import dt, AluOpType, AxisListType, ActivationFunctionType

N, K, V, A, R = 8, 4096, 8192, 4096, 512
HW = V + 8
BIG = 2097152.0
M4096, M64 = 1.5 * 2.0 ** 35, 1.5 * 2.0 ** 29
RVP, RVT, RVV, RHD = 0, 1, 2, 3
AW = A + 8
SRC = 512
FILL = [("c", 2304), ("v", 256), ("s", 1280), ("s", 256), ("g", 384), ("s", 1152), ("w", 512), ("s", 768), ("w", 768)]
CONVERT = [["hd"], ["vp", "vt"], [], []]
PIECES = [(0, K), (K, 6144), (6144, V)]
LOADS = [("copies", 0, FILL[0][1]), ("end", V, HW), ("vv", 0, K), ("hd", 0, K)]
LOADS += [(name, lo, hi) for lo, hi in PIECES for name in ("vp", "vt")]
LOADS.insert(-2, ("vv", K, V))
NS, W = 3, 8
COPY = ActivationFunctionType.Copy
ADD, SUB, MUL, MAX, MIN = AluOpType.add, AluOpType.subtract, AluOpType.mult, AluOpType.max, AluOpType.min
GE, LT, EQ, NE = AluOpType.is_ge, AluOpType.is_lt, AluOpType.is_equal, AluOpType.not_equal
AND = AluOpType.bitwise_and

SCRATCH = {}


def declare(where, dtype, **shapes):
    for n, s in shapes.items():
        SCRATCH[n] = (where, [128, s], dtype)


declare("sbuf", "float32", H=HW, AR=AW, RA=48, MU=128, MQ=16, MX=24, RST=32, OF=4, KF=4, TF=4, XF=4, SC=32, LL=512, RR=192,
        SND=48, RB=48, WW=16, SW=320, EYE=128, X0=384, XT0=384, QM=48, MM=48, SV=48, TH=48, TV=48, ANS=48,
        Y0=256, Y1=256, TLF=1280, CF=24, I160=160, PF=8)
declare("sbuf", "int32", RK=4, RT=4, KI=4, PI=2, TLI=1280)
declare("sbuf", "bfloat16", C96=32, C15=32, ZB=128, LTI=128, LTB=128, TWO=128, OH=56, EYB=128, SWB=320, CL=48, C2=48, C3=48)
declare("sbuf", "uint16", U0=4, U1=4, OFW=32, L0=24, LST0=16, LST1=16, LST2=16, AL0=16, AL1=16, AL2=16)
declare("psum", "float32", p0=512, p1=512, p2=512, p3=512, p4=512, pV=512, pm0=512)
SCRATCH["pm1"] = ("psum", [128, 32, 16], "float32")
for _s in ("h1", "h2", "h3", "a1", "a2", "a3", "a4"):
    SCRATCH["X" + _s] = ("sbuf", [128, NS, 272], "float32")
    SCRATCH["G" + _s] = ("sbuf", [128, 768], "float32")
    SCRATCH["h" + _s] = ("sbuf", [128, 48], "bfloat16")
    SCRATCH["e" + _s] = ("sbuf", [128, 48], "float32")
    if _s != "a1":
        SCRATCH["l" + _s] = ("sbuf", [128, 48], "uint16")
SCRATCH["TE"] = ("sbuf", [128, NS, 2 * W], "float32")
SCRATCH["AF"] = ("dram", [2, 8, A], "float32")
SCRATCH["OD"] = ("dram", [2, 128, 4], "uint16")
SEMAPHORES = ["v", "s", "t", "gp", "ldk", "ldt", "thd", "tvp", "tvt", "cast", "go", "ldh", "ldi", "lda", "od", "ow",
              "rK0", "rK1", "rK2", "lB", "rN0", "rN1", "rN2", "rT", "rC", "rV", "rF", "ownf", "wa0", "wa1", "st0", "st1"]


def readers(topo, cores, q):
    chips = [topo.chip(c) for c in cores]
    ring = [c for i, c in enumerate(chips) if c not in chips[:i]]
    at = [[r for r in range(N) if chips[r] == ring[(ring.index(chips[q]) + d) % len(ring)]] for d in range(len(ring))]
    mate = [r for r in at[0] if r != q]
    if chips[(q + 1) % N] == chips[q]:
        return at[1] + [q] + at[2] + mate + at[3]
    return at[2] + [q] + mate + at[1] + at[3]


def deal(topo, cores, me, dests):
    src = cores[me]
    far = [d for d in dests if topo.chip(cores[d]) != topo.chip(src)]
    es = topo.engines(src, cores[far[0]])
    per = len(es) // len(far)
    out = [(d, es[per * i:per * i + per]) for i, d in enumerate(far)]
    return out + [(d, [e for e in topo.engines(src, cores[d]) if e not in es][:per]) for d in dests if d not in far]


def asks(topo, cores, r, s):
    return deal(topo, cores, r, [q for q in range(N) if q != r and 3 * readers(topo, cores, q).index(r) // W == s])


def tells(topo, cores, z, s):
    return deal(topo, cores, z, [r for k, r in enumerate(readers(topo, cores, (z - 1) % N))
                                 if r != z and (3 * k + 2) // W == s])


def bits(es):
    m = 0
    for e in es:
        m |= 1 << e
    return m


def rank_program(g, core, T, topo):
    me = T.rank_of(core)
    if me is None:
        return
    cores = list(T.cores)
    prv, nxt = (me - 1) % N, (me + 1) % N
    q = {"v": g.vector, "s": g.scalar, "t": g.tensor, "y": g.sync, "g": g}
    cnt, seen = {}, {}

    def need(name, toks):
        for sem, val in toks:
            if seen.get((name, sem), 0) < val:
                q[name].wait_ge(T.sem[sem], val)
                seen[(name, sem)] = val

    def done(ins, sem, n):
        ins.then_inc(T.sem[sem], n)
        cnt[sem] = cnt.get(sem, 0) + n
        return (sem, cnt[sem])

    def tt(out, a, b, op, *toks):
        need("v", toks)
        return done(g.vector.tensor_tensor(out, a, b, op), "v", 1)

    def ts(out, a, s1, s2, o0, o1, *toks):
        need("v", toks)
        if o1 is None:
            return done(g.vector.tensor_scalar(out, a, s1, None, o0), "v", 1)
        return done(g.vector.tensor_scalar(out, a, s1, s2, o0, o1), "v", 1)

    def cp(out, a, *toks):
        need("v", toks)
        return done(g.vector.tensor_copy(out, a), "v", 1)

    def fill(ap, c, *toks):
        need("v", toks)
        return done(g.vector.memset(ap, c), "v", 1)

    def tr(out, a, *toks):
        need("v", toks)
        return done(g.vector.transpose(out, a), "v", 1)

    def act(out, a, *toks, bias=0.0):
        need("s", toks)
        return done(g.scalar.activation(out, a, COPY, bias=bias), "s", 1)

    def mm(out, l, r, start, stop, *toks):
        need("t", toks)
        return done(g.tensor.matmul(out, l, r, start, stop), "t", 1)

    def dma(name, out, src, sem, *toks):
        need(name, toks)
        return done(q[name].dma_start(out, src), sem, 16)

    def swap(out, src, mat, start, *toks, lo=0, hi=48, stop=False, view=None, into=None):
        tk = None
        for gs in range(2):
            for G in range(2):
                k = 160 * gs + 16 - 16 * (G - gs)
                tk = mm(into(gs) if into else out[:, lo + gs:hi:2], mat[:, k:k + 128], view(G) if view else src[:, lo + G:hi:2],
                        start and gs + G == 0, stop and gs + G == 2, *toks)
        return tk

    def same(out, src, mat, start, *toks, stop=False):
        return mm(out[:, 0:48], mat[:, :], src[:, 0:48], start, stop, *toks)

    def iota(out, pat, base, cm, **kw):
        return done(g.iota(out, pat, base, cm, **kw), "gp", 1)

    def pick(out, zero, pat, op, val, base, cm, *toks):
        need("g", toks)
        return done(g.affine_select(out, zero, pat, op, val, base, cm), "gp", 1)

    fl = {"allow_small_or_imprecise_dtypes": True}
    k_rk = dma("y", T.RK[:, :], T.rk[:, :], "ldk")
    k_rt = dma("s", T.RT[:, :], T.rt[:, :], "ldt")
    tiles = {"hd": (0, K), "vp": (256, V), "vt": (768, V)}

    def tile(buf, name, lo, hi, cl=None):
        c0, n = tiles[name]
        p0, h = 128 * lo // n, 64 * (hi - lo) // n
        if cl is None:
            return buf[p0:p0 + 2 * h, c0:c0 + n // 16]
        return buf[p0 + h * cl:p0 + h * cl + h, c0:c0 + n // 16]

    def fetch(name):
        for lo, hi in PIECES[:1] if name == "hd" else PIECES:
            k = dma("y", tile(T.TLI, name, lo, hi), T[name][:, lo:hi], "t" + name)
        return k

    k_tl = {name: fetch(name) for name in ("hd", "vp", "vt")}
    z0 = fill(T.ZB[:, :], 0.0)
    src0 = fill(T.H[:, V - 256:HW], 0.0)
    src1 = fill(T.H[:, V - SRC:V - 256], 0.0)
    i_q = iota(T.MQ[:, 8:16], [[4096, 8]], 0, 0, **fl)
    w = pick(T.LTI[:, :], T.ZB[:, :], [[-1, 128]], GE, 2.0, 0, 1, z0)
    i_c = iota(T.C96[:, :], [[0, 4], [96, 8]], 0, 0, **fl)
    i_l = pick(T.LTB[:, :], T.LTI[:, :], [[1, 128]], NE, -BIG, 0, -1, w)
    i_m = iota(T.MU[:, :], [[0, 4], [2, 32]], -31, 0, **fl)

    def shares(who):
        out, lo = [], 0
        for e, n in FILL:
            if e == who:
                out.append((lo, lo + n))
            lo += n
        return out

    filled = []
    for lo, hi in shares("g"):
        filled.append((lo, hi, iota(T.H[:, lo:hi], [[0, hi - lo]], 0, 0, **fl)))
    iota(T.I160[:, :], [[1, 160]], 0, 0, **fl)
    iota(T.PF[:, 0:2], [[1000, 2]], 16, 1, **fl)
    i_p = iota(T.PI[:, 0:1], [[1, 1]], 0, 1)

    fill(T.TWO[:, :], 2.0)
    fill(T.C15[:, :], -15.5)
    z2 = fill(T.OH[:, 0:24], 0.0)
    w = fill(T.RST[:, :], 1.0)
    k_cf = fill(T.CF[:, 16:24], BIG)
    fill(T.RST[:, 0:32:8], 0.0, w)
    k_mq = ts(T.MQ[:, 0:8], T.MQ[:, 8:16], M4096, None, ADD, None, i_q)
    for lo, hi in shares("v"):
        filled.append((lo, hi, fill(T.H[:, lo:hi], 0.0)))

    def sfill(lo, hi):
        while lo < hi:
            n = min(SRC if cnt.get("s") else 256, hi - lo)
            k = act(T.H[:, lo:lo + n], T.H[:, V - n:V], src1 if cnt.get("s") else src0)
            lo += n
        return k

    def convert(name):
        c0, n = tiles[name]
        return act(T.TLF[:, c0:c0 + n // 16], T.TLI[:, c0:c0 + n // 16], k_tl[name], bias=0.0 if name == "vt" else -float(V))

    s_c = {}
    for i, (lo, hi) in enumerate(shares("s")):
        filled.append((lo, hi, sfill(lo, hi)))
        for name in CONVERT[i]:
            s_c[name] = convert(name)
    filled.append((V - SRC, V, filled[-1][2]))

    k_of = ts(T.OF[:, :], T.RK[:, :], -2047.5, M4096, ADD, ADD, k_rk)
    w = ts(T.KI[:, :], T.RK[:, :], 4095, None, AND, None)
    mm(T.p0[:, 0:32], T.TWO[0:1, :], T.C96[0:1, :], True, False, z2, i_c)
    mm(T.p0[:, 0:32], T.TWO[0:1, :], T.C15[0:1, :], False, False)
    for f in range(4):
        k = ts(T.OH[:, 24 + 8 * f:32 + 8 * f], T.MQ[:, 0:8], T.OF[:, f:f + 1], None, EQ, None, k_of, k_mq)
        m = mm(T.p0[:, 0:32], (T.LTB if f == 3 else T.TWO)[:, :], T.OH[:, 8 * f:32 + 8 * f], False, f == 3, k, i_l)
    ts(T.TF[:, :], T.RT[:, :], 1.0, None, ADD, None, k_rt)
    cp(T.KF[:, :], T.KI[:, :], w)
    need("v", [m])
    w = done(g.vector.tensor_tensor_scan(T.SC[:, :], T.RST[:, :], T.p0[:, 0:32], 0.0, MUL, MIN), "v", 1)
    ts(T.MX[:, :], T.MU[:, 0:24], 32.0, 992.0 - BIG, MUL, ADD, i_m)
    k_xf = ts(T.XF[:, :], T.SC[:, 7:32:8], M64, M64, ADD, SUB, w)
    for f in range(4):
        for j, val in enumerate((T.KF, T.TF)):
            ts(T.RR[:, 48 * f + j:48 * f + 48:2], T.MX[:, :], T.XF[:, f:f + 1], val[:, f:f + 1], EQ, MUL, k_xf)
        w = ts(T.LL[:, 128 * f:128 * f + 128], T.MU[:, :], T.XF[:, f:f + 1], T.SC[:, 8 * f + 7:8 * f + 8], ADD, EQ)
        m = mm(T.p1[:, 0:48], T.LL[:, 128 * f:128 * f + 128], T.RR[:, 48 * f:48 * f + 48], f == 0, f == 3, w)
    k_snd = cp(T.SND[:, :], T.p1[:, 0:48], m)
    for lo, hi in shares("w"):
        filled.append((lo, hi, fill(T.H[:, lo:hi], 0.0)))
    cp(T.L0[:, 6:9], T.SND[:, 6 * me:6 * me + 6:2], k_snd)
    fill(T.CF[:, 8:16], float(A))
    k_ca = fill(T.AR[:, A:AW], 0.0)

    sent = [0]

    def spread(plan, src, dst, rsem, tok):
        need("g", [tok])
        trs = []
        for d, es in plan:
            rid, pid, _ = topo.addr(cores[d])
            trs.append(RemoteDMATransfer(dst_ids=[DstId(rid=rid, pnc=pid)], dma_engine_mask=bits(es), alu_op=0,
                                         remote_sem=T.sem[rsem], srcs=[src(d)], dsts=[dst(d)]))
            sent[0] += len(es)
        g.remote_dma_fused(trs, local_sem=T.sem.lB)

    def arrivals(calls, streams):
        return sum(len(es) for r in range(N) for s in streams for d, es in calls(topo, cores, r, s) if d == me)

    def slot(buf, q, r):
        k = readers(topo, cores, q).index(r)
        return buf[:, 6 * k:6 * k + 6]

    def ask(s):
        spread(asks(topo, cores, me, s), lambda d: T.SND[:, 6 * d:6 * d + 6], lambda d: slot(T.RB, d, me), "rK%d" % s, k_snd)

    ask(0)
    ask(1)
    r_k = [("rK%d" % s, arrivals(asks, [s])) for s in range(NS)]
    r_f = ("rF", arrivals(tells, range(NS)))

    w = ts(T.PI[:, 1:2], T.PI[:, 0:1], 16, None, AND, None, i_p)
    ts(T.EYE[:, :], T.I160[:, 16:144], T.PF[:, 0:1], None, EQ, None)
    w = cp(T.PF[:, 2:3], T.PI[:, 1:2], w)
    ts(T.PF[:, 3:4], T.PF[:, 2:3], 62.5, T.PF[:, 0:1], MUL, ADD, w)
    w = ts(T.PF[:, 4:5], T.PF[:, 2:3], -62.5, T.PF[:, 1:2], MUL, ADD)
    for gs in range(2):
        k_mat = ts(T.SW[:, 160 * gs:160 * gs + 160], T.I160[:, :], T.PF[:, 3 + gs:4 + gs], None, EQ, None, w)

    def scaled(out, mat):
        return ts(out, mat, -BIG, None, MUL, None, k_mat)

    def rows(win, lo, hi, src, row, sem, *toks):
        for gam in range(2):
            for cl in range(2):
                k = dma("s" if gam and hi == V else "y", win[16 * gam + row + 8 * cl:128:32, lo:hi], src(cl), sem, *toks)
        return k

    def cols(t, lo, hi):
        return lambda cl: t[4 * cl:4 * cl + 4, lo:hi]

    place = {"hd": RHD, "vp": RVP, "vt": RVT}
    for name, lo, hi in LOADS:
        sem = "ldh" if lo < K else "ldi"
        toks = [k for a, b, k in filled if a < hi and lo < b]
        if name == "copies":
            for r in range(RHD + 1, 8):
                k = dma("y", T.H[r:128:8, lo:hi], T.vv[:, 0:2 * (hi - lo)], sem)
        elif name == "vv":
            k = rows(T.H, lo, hi, cols(T.vv, lo, hi), RVV, sem, *toks)
        elif name == "end":
            k = dma("y", T.H[RVT:128:8, lo:hi], T.CF[0:16, 16:24], sem, k_cf)
        else:
            k = rows(T.H, lo, hi, lambda cl: tile(T.TLF, name, lo, hi, cl), place[name], sem, s_c[name], *toks)
        if lo < K:
            k_h0 = k
    k_h = k
    g.sync.sem_inc(T.sem.go, 1)
    g.scalar.sem_inc(T.sem.go, 1)
    need("g", [("go", 2)])
    ask(2)
    dma("g", T.AF[0], T.ap[:, :], "cast")
    k_cast = dma("g", T.AF[1], T.at[:, :], "cast")
    dma("y", T.AR[RVP:128:8, A:AW], T.CF[0:16, 8:16], "lda", k_ca)
    dma("y", T.AR[RVT:128:8, A:AW], T.CF[0:16, 16:24], "lda")
    need("y", [r_k[0]])
    for r in range(RVV + 1, 8):
        dma("y", T.AR[r:128:8, 0:A], T.vv[:, :], "lda")
    rows(T.AR, 0, A, cols(T.av, 0, A), RVV, "lda")
    rows(T.AR, 0, A, lambda cl: T.AF[0, 4 * cl:4 * cl + 4, :], RVP, "lda", k_cast)
    k_ar = rows(T.AR, 0, A, lambda cl: T.AF[1, 4 * cl:4 * cl + 4, :], RVT, "lda")

    def span(j, c=None):
        if j is None:
            return 0, 48
        return (16 * j, 16 * j + 16) if c is None else (16 * j + 8 * c, 16 * j + 8 * c + 8)

    def row(step, r, j=None, c=None):
        lo, hi = span(0, c)
        cut = slice(8 + r + 16 * lo, 8 + r + 16 * hi - 15, 16)
        return T["X" + step][:, :, cut] if j is None else T["X" + step][:, j, cut]

    def part(x, j=None, c=None):
        lo, hi = span(j, c)
        return x[:, lo:hi]

    got = {}

    def gather(step, j, *toks, c=None):
        lo, hi = span(j, c)
        win = T.H[:, 0:HW] if step[0] == "h" else T.AR[:, 0:AW]
        offs = T["AL%d" % j][:, :] if step == "a1" else T["l" + step][:, lo:hi]
        k = act(T["G" + step][:, 16 * lo:16 * hi], win.indirect(offs), *toks)
        for cc in range(2) if c is None else [c]:
            got[step, j, cc] = k

    def turn(step, j, c):
        lo, hi = span(j, c)
        return tr(T["X" + step][:, j, 136 * c:136 * c + 128], T["G" + step][:, 16 * lo:16 * hi], got[step, j, c])

    def nextlist(step, then, j, k):
        add, cap = (float(V), float(V)) if step[0] == "h" else (0.0, float(A))
        k = ts(part(T["l" + then], j), row(step, RVP, j), add, cap, ADD, MIN, k)
        for c in range(2) if (then, j) == ("a4", NS - 1) else [None]:
            gather(then, j, k, c=c)

    def stops(step, open_t, *toks, j=None):
        return tt(part(T["h" + step], j), row(step, RVT, j), part(open_t, j), LT, *toks)

    def gives(step, *toks, j=None):
        return tt(part(T["e" + step], j), part(T["h" + step], j), row(step, RVV, j), MUL, *toks)

    def walk(slots, then=None):
        turn(slots[0][0], slots[0][1], 0)
        for n, (step, j, after, fillers) in enumerate(slots):
            k = turn(step, j, 1)
            nx = slots[n + 1][:2] if n + 1 < len(slots) else then
            if nx and step != "h3":
                turn(nx[0], nx[1], 0)
            for f in fillers:
                f()
            after(j, k)
            if nx and step == "h3":
                turn(nx[0], nx[1], 0)

    S = {}

    def keys(j):
        lo, hi = ((0, 6), (9, 16), (16, 24))[j]
        return cp(T.L0[:, lo:hi], T.RB[:, 2 * lo:2 * hi:2], r_k[j])

    def first(j, k):
        return act(T.X0[:, 128 * j:128 * j + 128], T.H[:, 0:K].indirect(T.L0[:, 8 * j:8 * j + 8]), k)

    def turned(j, *toks):
        return tr(T.XT0[:, 128 * j:128 * j + 128], T.X0[:, 128 * j:128 * j + 128], *toks)

    def heads(j, w):
        for c in range(2):
            a = 128 * j + RHD + 8 * (1 - c)
            k = ts(part(T.lh1, j, c), T.XT0[:, a:a + 113:16], float(V), float(V), ADD, MIN, w)
        for c in range(2 if j == NS - 1 else 0):
            a = RHD + 8 * (1 - c)
            S["t0"] = swap(None, None, T.SW, c == 0, w, k_mat, stop=c == 1, view=lambda G: T.XT0[:, a + 16 * G:a + 369:32],
                           into=lambda gs: T.pm1[:, 0:NS, 8 * c + gs:8 * c + 8:2])
        return k

    k = keys(0)
    w = turned(0, act(T.X0[:, 64:128], T.H[:, 0:K].indirect(T.L0[:, 4:8]), k, k_h0),
               cp(T.X0[:, 0:64], T.H[:, 0:K].indirect(T.L0[:, 0:4]), k, k_h0))
    f1 = first(1, keys(1))
    gather("h1", 0, heads(0, w), k_h)
    k_own = cp(T.RB[:, 13:18:2], T.SND[:, 6 * me + 1:6 * me + 6:2])
    scaled(T.EYB[:, :], T.EYE[:, :])
    w = turned(1, f1)
    f2 = first(2, keys(2))
    gather("h1", 1, heads(1, w))
    scaled(T.SWB[:, 0:160], T.SW[:, 0:160])
    turn("h1", 0, 0)
    k = turn("h1", 0, 1)
    w = turned(2, f2)
    k = ts(part(T.lh2, 0), row("h1", RVP, 0), float(V), float(V), ADD, MIN, k)
    gather("h1", 2, heads(2, w))
    gather("h2", 0, k)
    turn("h1", 1, 0)
    k = turn("h1", 1, 1)
    for c in range(2):
        k_te = cp(T.TE[:, :, 8 * c:8 * c + 8], T.RB[:, 1:48:2], k_own)
    nextlist("h1", "h2", 1, k)
    scaled(T.SWB[:, 160:320], T.SW[:, 160:320])

    zc = cores[nxt]
    rid, pid, _ = topo.addr(zc)
    far_n = min(len(topo.engines(cores[r], cores[(r + 1) % N])) for r in range(N))
    es_d = topo.engines(core, zc)[:far_n]

    def onward(dst, src, rsem, tok):
        need("g", [tok])
        g.remote_dma(dst, src, T.sem[rsem], T.sem.lB, pid, rid, bits(es_d))
        sent[0] += far_n
        return (rsem, far_n)

    r_t = onward(T.TH[:, :], T.TE[:, :, :], "rT", k_te)
    swap(T.p2, None, T.SW, True, k_te, view=lambda G: T.TE[:, :, G:16:2])

    def stops1():
        k = tt(T.hh1[:, :], row("h1", RVT), T.TE[:, :, :], LT)
        S["t2"] = swap(T.p2, T.hh1, T.SWB, False, k, stop=True)

    def stops2():
        mm(T.p3[:, 0:48], T.EYE[:, :], T.TE[:, :, :], True, False)
        same(T.p3, T.hh1, T.EYB, False)
        same(T.p4, T.hh1, T.EYB, True)
        S["t3"] = swap(T.p3, T.hh2, T.SWB, False, stops("h2", T.p2, S["t2"]), stop=True)
        S["t4"] = swap(T.p4, T.hh2, T.SWB, False, stop=True)

    def closed():
        ts(T.CL[:, :], T.p4[:, 0:48], -1.0 / BIG, None, MUL, None, S["t4"])

    pm, r_n = {1: (T.pm0, 0, 2), 2: (T.p0, 2, 3)}, []

    def larger():
        S["qm"] = tt(T.QM[:, :], row("h1", RVP), T.pm1[:, 0:NS, :], MAX, S["t0"])

    def second(j, k):
        if j in pm:
            bank, lo, hi = pm[j]
            S["pm", j] = swap(bank, None, T.SW, True, k, lo=16 * lo, hi=16 * hi, stop=True,
                              view=lambda G: T.Xh2[:, lo:hi, 8 + RVP + 16 * G:8 + RVP + 241:32])
        nextlist("h2", "h3", j, k)

    def largest(j):
        def call():
            bank, lo, hi = pm[j]
            k = tt(T.MM[:, 16 * lo:16 * hi], T.QM[:, 16 * lo:16 * hi], bank[:, 16 * lo:16 * hi], MAX, S["pm", j], S["qm"])
            for i in range(lo, hi):
                S["mm", i] = k
        return call

    def leave(j, k):
        w = tt(T["LST%d" % j][:, :], row("h3", RVP, j), part(T.MM, j), MAX, k, S["mm", j])
        r_n.append(onward(T["AL%d" % j][:, :], T["LST%d" % j][:, :], "rN%d" % j, w))

    walk([("h1", 2, lambda j, k: nextlist("h1", "h2", j, k), []),
          ("h2", 0, second, [stops1]), ("h2", 1, second, []), ("h2", 2, second, [larger]),
          ("h3", 0, leave, [largest(1), stops2]), ("h3", 1, leave, [largest(2)]), ("h3", 2, leave, [closed])])
    k_h3 = stops("h3", T.p3, S["t3"])
    gives("h1")
    r_c = onward(T.C3[:, :], T.C2[:, :], "rC", tt(T.C2[:, :], T.CL[:, :], T.hh3[:, :], MAX, k_h3))
    swap(T.pV, T.eh2, T.SW, True, gives("h2"))
    t_v = same(T.pV, T.eh1, T.EYE, False, stop=True)
    gives("h3")
    w = tt(T.WW[:, 0:4], T.SC[:, 7:32:8], T.XF[:, :], SUB)
    ts(T.WW[:, 4:8], T.XF[:, :], BIG, 1.0 / 32, ADD, MUL)
    w = ts(T.WW[:, 8:12], T.WW[:, 0:4], 31.0, 24.0, ADD, MUL, w)
    w = tt(T.WW[:, 12:16], T.WW[:, 4:8], T.WW[:, 8:12], ADD, w)
    ts(T.U0[:, :], T.WW[:, 12:16], 0.0, None, ADD, None, w)
    k_u = ts(T.U1[:, :], T.WW[:, 12:16], 1.0, None, ADD, None)
    r_v = onward(T.TV[:, :], T.SV[:, :], "rV", tt(T.SV[:, :], T.eh3[:, :], T.pV[:, 0:48], ADD, t_v))
    dma("y", T.OD[0], T.U0[:, :], "od", k_u)
    k_od = dma("y", T.OD[1], T.U1[:, :], "od")
    for gr in range(8):
        k_ow = dma("y", T.OFW[16 * gr:16 * gr + 16, :], T.OD[gr // 4], "ow", k_od)

    for src, one, other, tok in ((T.TH, T.EYE, T.SW, r_t), (T.C3, T.EYB, T.SWB, r_c)):
        t_1 = swap(T.p1, src, other, src is T.TH, tok, k_h3, stop=src is T.C3)
        same(T.p2, src, one, src is T.TH)
        swap(T.p3, src, other, src is T.TH)
        same(T.p4, src, one, src is T.TH)

    def a_stops1():
        S["h1"] = stops("a1", T.p1, t_1)
        S["t2"] = swap(T.p2, T.ha1, T.SWB, False, S["h1"], stop=True)
        same(T.p3, T.ha1, T.EYB, False)
        swap(T.p4, T.ha1, T.SWB, False)

    def a_gives1():
        swap(T.pV, T.ea1, T.SW, True, gives("a1", S["h1"]))

    def a_stops2():
        S["h2"] = stops("a2", T.p2, S["t2"])
        S["t3"] = swap(T.p3, T.ha2, T.SWB, False, S["h2"], stop=True)
        same(T.p4, T.ha2, T.EYB, False)

    def a_gives2():
        same(T.pV, T.ea2, T.EYE, False, gives("a2", S["h2"]))
        same(T.pV, T.TV, T.EYE, False, r_v)

    for j in range(NS):
        gather("a1", j, r_n[j], k_ar)
    fillers = {("a2", 1): [a_stops1], ("a2", 2): [a_gives1], ("a3", 0): [a_stops2], ("a3", 1): [a_gives2]}
    walk([(step, j, lambda j, k, step=step, then=then: nextlist(step, then, j, k), fillers.get((step, j), []))
          for step, then in (("a1", "a2"), ("a2", "a3"), ("a3", "a4")) for j in range(NS)], then=("a4", 0))
    h3 = stops("a3", T.p3, S["t3"])
    t_4 = swap(T.p4, T.ha3, T.SWB, False, h3, stop=True)

    def answer(j, c, *toks):
        return tt(T.ANS[:, 16 * j + 1 - c:16 * j + 16:2], part(T.ea4, j, c), part(T.pV, j, c), ADD, t_v, *toks)

    def tell(j, k):
        spread(tells(topo, cores, me, j), lambda d: slot(T.ANS, prv, d), lambda d: T.RA[:, 6 * prv:6 * prv + 6], "rF", k)

    k = turn("a4", 0, 1)
    t_v = swap(T.pV, T.ea3, T.SW, False, gives("a3", h3), stop=True)
    turn("a4", 1, 0)
    h0 = stops("a4", T.p4, t_4, k, j=0)
    k = turn("a4", 1, 1)
    e0 = gives("a4", h0, j=0)
    turn("a4", 2, 0)
    h1 = stops("a4", T.p4, k, j=1)
    k = turn("a4", 2, 1)
    e1 = gives("a4", h1, j=1)
    answer(0, 0, e0)
    tell(0, answer(0, 1))
    h2 = stops("a4", T.p4, k, j=2)
    answer(1, 0, e1)
    tell(1, answer(1, 1))
    answer(2, 0, gives("a4", h2, j=2))
    k_ans = answer(2, 1)
    tell(2, k_ans)

    k_of2 = dma("y", T.RA[:, 6 * prv:6 * prv + 6], slot(T.ANS, prv, me), "ownf", k_ans)
    ends = []
    for cl, nm in ((0, "y"), (1, "s")):
        ends.append(dma(nm, T.H[64 * cl:64 * cl + 64:16, 0:1536], T.RA[:, :], "wa%d" % cl, r_f, k_of2))
    need("v", ends + [k_ow])
    yv = done(g.vector.tensor_copy(T.Y0[:, :], T.H[:, 0:1536].indirect(T.OFW[:, 0:16])), "v", 1)
    ys = act(T.Y1[:, :], T.H[:, 0:1536].indirect(T.OFW[:, 16:32]), *(ends + [k_ow]))
    dma("y", T.y[:, 0:256], T.Y0[0:128:16, :], "st0", yv)
    dma("s", T.y[:, 256:512], T.Y1[0:128:16, :], "st1", ys)
    need("g", [("lB", sent[0]), r_t, r_c, r_v, r_f] + r_n + r_k + list(cnt.items()))
